import numpy as np
import ml_dtypes


def mxq(x, axis, fmt="e4m3"):
    dtype, down = {"e4m3": (ml_dtypes.float8_e4m3fn, 7), "e5m2": (ml_dtypes.float8_e5m2, 14)}[fmt]
    v = np.moveaxis(np.asarray(x, np.float32).astype(ml_dtypes.bfloat16).astype(np.float64), axis, -1)
    blocks = v.reshape(v.shape[:-1] + (-1, 32))
    amax = np.abs(blocks).max(-1, keepdims=True)
    byte = np.maximum(np.where(amax > 0, np.frexp(amax)[1] - 1 + 127, 0) - down, 1)
    scale = np.exp2(byte - 127.0)
    codes = (blocks / scale).astype(np.float32).astype(dtype).astype(np.float64)
    return np.moveaxis((codes * scale).reshape(v.shape), -1, axis)


WIDE = False


def mx_kscale(k):
    if not WIDE:
        return np.ones(k)
    levels = np.array([10, -10, 5, -5, 0])
    if k % 512:
        return np.exp2(np.random.permutation(np.resize(levels, k // 32))).repeat(32)
    a = np.empty((k // 512, 16))
    for p in range(k // 512):
        a[p, :8] = np.random.permutation(np.resize(levels, 8))
        for g in range(8):
            far = levels[np.abs(levels - a[p, g]) >= 10]
            a[p, g + 8] = far[np.random.randint(len(far))]
    return np.exp2(a.ravel()).repeat(32)


def f64(x):
    return np.asarray(x).astype(np.float64)


def striped(idx):
    return np.tile(idx.reshape(-1, 16).T, (8, 1)).astype(np.uint16)


def unstriped(offs):
    return offs[:16].T.reshape(-1).astype(np.int64)


E2M1 = np.array([0.0, 0.5, 1.0, 1.5, 2.0, 3.0, 4.0, 6.0, -0.0, -0.5, -1.0, -1.5, -2.0, -3.0, -4.0, -6.0])


def pack_weight(w, fmt):
    k, n = w.shape
    w = f64(np.asarray(w, np.float32).astype(ml_dtypes.bfloat16)).reshape(k // 32, 32, n)
    amax = np.abs(w).max(1)
    if fmt == "e4m3":
        byte = np.frexp(amax)[1] - 1 + 127 - 7
    else:
        mant, ex = np.frexp(amax / 6.0)
        byte = np.where(mant > 0.5, ex, ex - 1) + 127
    byte = np.clip(np.where(amax > 0, byte, 1), 1, 254)
    scaled = (w * np.exp2(127.0 - byte)[:, None, :]).reshape(k, n).astype(np.float32)
    by_word = np.ascontiguousarray(scaled.reshape(k // 512, 128, 4, n).transpose(0, 1, 3, 2))
    if fmt == "e4m3":
        words = by_word.astype(ml_dtypes.float8_e4m3fn).view(np.uint8)
    else:
        c = by_word.astype(ml_dtypes.float4_e2m1fn).view(np.uint8) & 0xF
        words = (c[..., 0::2] | (c[..., 1::2] << 4)).reshape(k // 512, 128, 2 * n)
    return np.ascontiguousarray(words), np.ascontiguousarray(byte.astype(np.uint8).reshape(k // 512, 16, n))


def unpack_weight(words, scales, fmt):
    g, _, n = scales.shape
    words = np.ascontiguousarray(words).reshape(g, 128, n, -1)
    if fmt == "e4m3":
        vals = words.view(ml_dtypes.float8_e4m3fn).astype(np.float64)
    else:
        nib = np.empty((g, 128, n, 4), np.uint8)
        nib[..., 0::2] = words & 0xF
        nib[..., 1::2] = words >> 4
        vals = E2M1[nib]
    vals = vals * np.repeat(np.exp2(scales.astype(np.float64) - 127.0), 8, axis=1)[..., None]
    return vals.transpose(0, 1, 3, 2).reshape(g * 512, n)


def gelu(v):
    return 0.5 * v * (1.0 + np.tanh(np.sqrt(2.0 / np.pi) * (v + 0.044715 * v**3)))


K, H, N, T, S, T2 = 1024, 512, 768, 2048, 1024, 2048

def setup_inputs():
    n = np.random.standard_normal
    s = mx_kscale(K)[:, None]
    u = mx_kscale(H)[:, None]
    tab_words, tab_scales = pack_weight(n((K, T)) * s, "e4m3")
    wg_words, wg_scales = pack_weight(1.5 * n((K, H)) / np.sqrt(K) / s, "e2m1")
    return {
        "tab_words": tab_words,
        "tab_scales": tab_scales,
        "offs": striped(np.random.permutation(T)[:S]),
        "wv": (2.0 * n((K, H)) / np.sqrt(K) / s).astype(np.float32),
        "wg_words": wg_words,
        "wg_scales": wg_scales,
        "offs2": striped(np.random.permutation(T2)[:S]),
        "wgs": np.exp(0.3 * n((128, S))).astype(np.float32),
        "base": (n((H, T2)) * u).astype(np.float32),
        "wo": (n((H, N)) / np.sqrt(H) / u).astype(np.float32),
    }

def reference(tab_words, tab_scales, offs, wv, wg_words, wg_scales, offs2, wgs, base, wo):
    v = unpack_weight(tab_words, tab_scales, "e4m3")[:, unstriped(offs)]
    a = mxq(f64(wv), 0, "e4m3").T @ v
    b = unpack_weight(wg_words, wg_scales, "e2m1").T @ v
    h = a * (1.0 / (1.0 + np.exp(-b)))
    page = np.zeros((H, T2))
    page[:, unstriped(offs2)] = np.tile(f64(wgs), (H // 128, 1)) * h
    z = f64(base) / np.sqrt(1.0 + page * page)
    return mxq(f64(wo), 0, "e4m3").T @ mxq(z, 0, "e4m3")

@@ -1,0 +1,290 @@
+from contextlib import ExitStack
+
+import concourse.mybir as mybir
+
+K, H, N, T, S, T2 = 1024, 512, 768, 2048, 1024, 2048
+FLOPS = 2 * (2 * K * H * S + H * N * T2)
+
+F32 = mybir.dt.float32
+BF16 = mybir.dt.bfloat16
+I32 = mybir.dt.int32
+U32 = mybir.dt.uint32
+U16 = mybir.dt.uint16
+U8 = mybir.dt.uint8
+FP8X4 = mybir.dt.float8_e4m3fn_x4
+FP4X4 = mybir.dt.float4_e2m1fn_x4
+ACT = mybir.ActivationFunctionType
+MULT = mybir.AluOpType.mult
+
+P = 128
+PACK = 4
+PASSES = K // (P * PACK)
+HALF = S // 2
+BANK = 512
+CHUNKS = (256, 256, 512, 512, 512)
+VECTOR_BANKS = (0, 0, 0, 1, 4)
+
+
+def tile_list_landmark_gated_damping_kernel(
+    tc, tab_words, tab_scales, offs, wv, wg_words, wg_scales, offs2, wgs, base, wo, out
+):
+    nc = tc.nc
+    with ExitStack() as ctx:
+        lists = ctx.enter_context(tc.tile_pool(name="lists", bufs=1))
+        keep = ctx.enter_context(tc.tile_pool(name="keep", bufs=1))
+        ring = ctx.enter_context(tc.tile_pool(name="ring", bufs=2))
+        stage = ctx.enter_context(tc.tile_pool(name="stage", bufs=5))
+        psum = ctx.enter_context(tc.psum_pool(name="psum", bufs=8))
+
+        def held(shape, dtype, name):
+            return keep.tile(shape, dtype, name=name, align_bytes=64)
+
+        picks = lists.tile([P, S // 16], U16, name="picks")
+        places = lists.tile([P, S // 16], U16, name="places")
+
+        tab_w = [held([P, T], I32, f"tab_w{a}") for a in range(PASSES)]
+        tab_s = held([P, PASSES, T // 4], I32, "tab_s")
+        wg_raw_w = held([P, PASSES, H // 2], I32, "wg_raw_w")
+        wg_raw_s = held([P, PASSES, H // 4], I32, "wg_raw_s")
+        wv_raw = [held([P, PACK, H], F32, f"wv_raw{a}") for a in range(PASSES)]
+        wgs_first = held([P, S], F32, "wgs_first")
+        wgs_rest = held([P, PACK - 1, S], F32, "wgs_rest")
+        wo_raw = held([P, PACK, N], F32, "wo_raw")
+        starts = [sum(CHUNKS[:c]) for c in range(len(CHUNKS))]
+        base_c = [held([P, PACK, w], F32, f"base{c}") for c, w in enumerate(CHUNKS)]
+        damp_c = [held([P, PACK, w], F32, f"damp{c}") for c, w in enumerate(CHUNKS)]
+        pages = [held([P, T2], F32, f"page{i}") for i in range(2)]
+        warm = held([P, 2], F32, "warm")
+
+        nc.vector.memset(tab_s[:], 0)
+        nc.vector.memset(wg_raw_s[:], 0)
+        nc.vector.memset(warm[:, 0:1], 0.0)
+        nc.scalar.activation(warm[:, 1:2], warm[:, 0:1], ACT.Sigmoid)
+        for page in pages:
+            nc.vector.memset(page[:], 0.0)
+
+        def load_words(a):
+            nc.sync.dma_start(tab_w[a][:], tab_words[a].rearrange("p t i -> p (t i)").bitcast(I32))
+
+        def load_wv(a):
+            rows = wv[a * P * PACK : (a + 1) * P * PACK, :]
+            nc.sync.dma_start(wv_raw[a][:], rows.rearrange("(p j) c -> p j c", j=PACK))
+
+        def load_scales(tile, scales):
+            for q in range(4):
+                nc.sync.dma_start(
+                    tile[32 * q : 32 * q + 4, :, :],
+                    scales.bitcast(I32)[:, 4 * q : 4 * q + 4, :].rearrange("a r w -> r a w"),
+                )
+
+        quadrants = (0, 2, 1, 3)
+        wgs_rows = wgs.rearrange("(m t) j -> m t j", t=PACK)
+        nc.sync.dma_start(picks[:], offs)
+        load_words(0)
+        load_scales(tab_s, tab_scales)
+        nc.sync.dma_start(wg_raw_w[:], wg_words.bitcast(I32).rearrange("a p w -> p a w"))
+        load_wv(0)
+        load_scales(wg_raw_s, wg_scales)
+        load_words(1)
+        load_wv(1)
+        nc.sync.dma_start(places[:], offs2)
+        for q in quadrants:
+            nc.sync.dma_start(wgs_first[32 * q : 32 * q + 32, :], wgs_rows[:, 0, :])
+        for q in quadrants:
+            nc.sync.dma_start(wgs_rest[32 * q : 32 * q + 32, :, :], wgs_rows[:, 1:, :])
+        nc.sync.dma_start(wo_raw[:], wo.rearrange("(p j) n -> p j n", j=PACK))
+        base_rows = base.rearrange("(p j) t -> p j t", j=PACK)
+        for c, w in enumerate(CHUNKS):
+            nc.sync.dma_start(base_c[c][:], base_rows[:, :, starts[c] : starts[c] + w])
+
+        key_w = [[held([P, HALF], U32, f"key_w{a}_{s}") for s in range(2)] for a in range(PASSES)]
+        key_s = [[held([P, HALF], U8, f"key_s{a}_{s}") for s in range(2)] for a in range(PASSES)]
+
+        def half_of(offsets, s):
+            return offsets[:, s * HALF // 16 : (s + 1) * HALF // 16]
+
+        def gather_words(a, s):
+            nc.vector.tensor_copy(key_w[a][s][:], tab_w[a][:].bitcast(U32).indirect(half_of(picks, s)))
+
+        def gather_scales(a, s):
+            nc.vector.tensor_copy(key_s[a][s][:], tab_s[:, a, :].bitcast(U8).indirect(half_of(picks, s)))
+
+        wg_w = held([P, PASSES, H], U16, "wg_w")
+        wg_s = held([P, PASSES, H], U8, "wg_s")
+
+        def permute_wg():
+            nc.vector.tensor_copy(
+                wg_w[:].rearrange("p a (t m) -> p a t m", t=PACK),
+                wg_raw_w[:].bitcast(U16).rearrange("p a (m t) -> p a t m", t=PACK),
+            )
+            nc.vector.tensor_copy(
+                wg_s[:].rearrange("p a (t m) -> p a t m", t=PACK),
+                wg_raw_s[:].bitcast(U8).rearrange("p a (m t) -> p a t m", t=PACK),
+            )
+
+        wv_bf = [held([P, PACK, P, PACK], BF16, f"wv_bf{a}") for a in range(PASSES)]
+        wv_w = [held([P, H], U32, f"wv_w{a}") for a in range(PASSES)]
+        wv_s = [held([P, H], U8, f"wv_s{a}") for a in range(PASSES)]
+
+        def round_wv(a, t0, t1):
+            nc.scalar.activation(
+                wv_bf[a][:, t0:t1, :, :].rearrange("p t m j -> p m j t"),
+                wv_raw[a][:].rearrange("p j (m t) -> p m j t", t=PACK)[:, :, :, t0:t1],
+                ACT.Copy,
+            )
+
+        def quantize_wv(a, t0, t1):
+            cols = slice(t0 * P, t1 * P)
+            nc.vector.quantize_mx(
+                out=wv_w[a][:, cols].bitcast(FP8X4),
+                scales=wv_s[a][:, cols],
+                in_=wv_bf[a][:, t0:t1, :, :].rearrange("p t m j -> p (t m j)"),
+            )
+
+        gated = [held([P, S], F32, f"gated{t}") for t in range(PACK)]
+
+        def gate(t, s):
+            cols = slice(t * P, (t + 1) * P)
+            acc = psum.tile([P, BANK], F32, name="acc")
+            for a in range(PASSES):
+                nc.tensor.matmul_mx(
+                    out=acc[:],
+                    lhsT=wg_w[:, a, cols].bitcast(FP4X4),
+                    lhsT_scale=wg_s[:, a, cols],
+                    rhs=key_w[a][s][:].bitcast(FP8X4),
+                    rhs_scale=key_s[a][s][:],
+                    start=(a == 0),
+                    stop=(a == PASSES - 1),
+                )
+            nc.scalar.activation(gated[t][:, s * HALF : (s + 1) * HALF], acc[:], ACT.Sigmoid)
+
+        def value(t, s):
+            cols = slice(t * P, (t + 1) * P)
+            acc = psum.tile([P, BANK], F32, name="acc")
+            for a in range(PASSES):
+                nc.tensor.matmul_mx(
+                    out=acc[:],
+                    lhsT=wv_w[a][:, cols].bitcast(FP8X4),
+                    lhsT_scale=wv_s[a][:, cols],
+                    rhs=key_w[a][s][:].bitcast(FP8X4),
+                    rhs_scale=key_s[a][s][:],
+                    start=(a == 0),
+                    stop=(a == PASSES - 1),
+                )
+            half = gated[t][:, s * HALF : (s + 1) * HALF]
+            nc.vector.tensor_tensor(half, acc[:], half, MULT)
+
+        def scatter(t, s0, s1):
+            cols = slice(s0 * HALF, s1 * HALF)
+            weights = wgs_first[:, cols] if t == 0 else wgs_rest[:, t - 1, cols]
+            offsets = places[:, s0 * HALF // 16 : s1 * HALF // 16]
+            nc.vector.tensor_tensor(pages[t % 2][:].indirect(offsets), gated[t][:, cols], weights, MULT)
+
+        def damp(t, c):
+            factor = damp_c[c][:, t, :]
+            nc.scalar.activation(factor, pages[t % 2][:, starts[c] : starts[c] + CHUNKS[c]], ACT.Square)
+            nc.scalar.activation(factor, factor, ACT.Abs_reciprocal_sqrt, bias=1.0)
+
+        round_wv(0, 0, PACK)
+        round_wv(1, 0, 1)
+        round_wv(1, 1, PACK)
+        gather_words(0, 0)
+        gather_scales(0, 0)
+        gather_scales(1, 0)
+        permute_wg()
+        quantize_wv(0, 0, PACK)
+        gather_words(1, 0)
+        quantize_wv(1, 0, 1)
+        gate(0, 0)
+        gather_words(0, 1)
+        gather_scales(0, 1)
+        gather_scales(1, 1)
+        gather_words(1, 1)
+        value(0, 0)
+        gate(0, 1)
+        quantize_wv(1, 1, 2)
+        quantize_wv(1, 2, PACK)
+        scatter(0, 0, 1)
+        value(0, 1)
+        for t in range(1, PACK):
+            gate(t, 0)
+            gate(t, 1)
+        value(1, 0)
+        scatter(0, 1, 2)
+        value(1, 1)
+
+        wo_bf = held([P, N, PACK], BF16, "wo_bf")
+        wo_w = held([P, N], U32, "wo_w")
+        wo_s = held([P, N], U8, "wo_s")
+        nc.scalar.activation(
+            wo_bf[:].rearrange("p (c i) j -> p c j i", i=4),
+            wo_raw[:].rearrange("p j (c i) -> p c j i", i=4),
+            ACT.Copy,
+        )
+
+        for t in range(1, PACK):
+            for c in range(len(CHUNKS)):
+                damp(t - 1, c)
+            if t + 1 < PACK:
+                value(t + 1, 0)
+                value(t + 1, 1)
+            scatter(t, 0, 2)
+
+        for n0, n1 in ((0, 512), (512, N)):
+            nc.vector.quantize_mx(
+                out=wo_w[:, n0:n1].bitcast(FP8X4),
+                scales=wo_s[:, n0:n1],
+                in_=wo_bf[:, n0:n1, :].rearrange("p n j -> p (n j)"),
+            )
+
+        out_rows = out.rearrange("(n p) t -> p n t", p=P)
+
+        def states(c):
+            w = CHUNKS[c]
+            damp(PACK - 1, c)
+            z_bf = ring.tile([P, w, PACK], BF16, name="z_bf", align_bytes=64)
+            z_w = ring.tile([P, w], U32, name="z_w", align_bytes=64)
+            z_s = ring.tile([P, w], U8, name="z_s", align_bytes=64)
+            nc.vector.tensor_tensor(
+                z_bf[:].rearrange("p (c i) j -> p c j i", i=4),
+                base_c[c][:].rearrange("p j (c i) -> p c j i", i=4),
+                damp_c[c][:].rearrange("p j (c i) -> p c j i", i=4),
+                MULT,
+            )
+            nc.vector.quantize_mx(
+                out=z_w[:].bitcast(FP8X4), scales=z_s[:], in_=z_bf[:].rearrange("p c j -> p (c j)")
+            )
+            return z_w, z_s
+
+        def project(c, z_w, z_s):
+            w = CHUNKS[c]
+            per_bank = BANK // w
+            banks = N // P // per_bank
+            for n0 in range(0, N // P, 2):
+                result = stage.tile([P, 2, w], F32, name="result")
+                for n1 in range(n0, n0 + 2, per_bank):
+                    acc = psum.tile([P, per_bank, w], F32, name="acc")
+                    for i in range(per_bank):
+                        cols = slice((n1 + i) * P, (n1 + i + 1) * P)
+                        nc.tensor.matmul_mx(
+                            out=acc[:, i, :],
+                            lhsT=wo_w[:, cols].bitcast(FP8X4),
+                            lhsT_scale=wo_s[:, cols],
+                            rhs=z_w[:].bitcast(FP8X4),
+                            rhs_scale=z_s[:],
+                            start=True,
+                            stop=True,
+                        )
+                    part = result[:, n1 - n0 : n1 - n0 + per_bank, :]
+                    bank = n1 // per_bank
+                    if (bank + 1) * VECTOR_BANKS[c] // banks > bank * VECTOR_BANKS[c] // banks:
+                        nc.vector.tensor_copy(part, acc[:])
+                    else:
+                        nc.scalar.copy(part, acc[:])
+                nc.sync.dma_start(out_rows[:, n0 : n0 + 2, starts[c] : starts[c] + w], result[:])
+
+        made = states(0)
+        for c in range(len(CHUNKS)):
+            ahead = states(c + 1) if c + 1 < len(CHUNKS) else None
+            project(c, *made)
+            made = ahead

@@ -21,8 +21,8 @@ PACK = 4
 PASSES = K // (P * PACK)
 HALF = S // 2
 BANK = 512
-CHUNKS = (256, 256, 512, 512, 512)
-VECTOR_BANKS = (0, 0, 0, 1, 4)
+CHUNKS = (128, 128, 256, 512, 512, 256, 256)
+VECTOR_BANKS = (0, 0, 0, 1, 2, 1, 2)
 
 
 def tile_list_landmark_gated_damping_kernel(
@@ -47,12 +47,11 @@ def tile_list_landmark_gated_damping_kernel(
         wg_raw_w = held([P, PASSES, H // 2], I32, "wg_raw_w")
         wg_raw_s = held([P, PASSES, H // 4], I32, "wg_raw_s")
         wv_raw = [held([P, PACK, H], F32, f"wv_raw{a}") for a in range(PASSES)]
-        wgs_first = held([P, S], F32, "wgs_first")
-        wgs_rest = held([P, PACK - 1, S], F32, "wgs_rest")
+        weights = [held([P, S], F32, f"weights{t}") for t in range(PACK)]
         wo_raw = held([P, PACK, N], F32, "wo_raw")
         starts = [sum(CHUNKS[:c]) for c in range(len(CHUNKS))]
-        base_c = [held([P, PACK, w], F32, f"base{c}") for c, w in enumerate(CHUNKS)]
-        damp_c = [held([P, PACK, w], F32, f"damp{c}") for c, w in enumerate(CHUNKS)]
+        base_sb = held([P, PACK, T2], F32, "base_sb")
+        factors = held([P, PACK, T2], F32, "factors")
         pages = [held([P, T2], F32, f"page{i}") for i in range(2)]
         warm = held([P, 2], F32, "warm")
 
@@ -77,25 +76,26 @@ def tile_list_landmark_gated_damping_kernel(
                     scales.bitcast(I32)[:, 4 * q : 4 * q + 4, :].rearrange("a r w -> r a w"),
                 )
 
-        quadrants = (0, 2, 1, 3)
-        wgs_rows = wgs.rearrange("(m t) j -> m t j", t=PACK)
-        nc.sync.dma_start(picks[:], offs)
-        load_words(0)
-        load_scales(tab_s, tab_scales)
+        def load_weights(t, cols):
+            rows = wgs.rearrange("(m t) j -> m t j", t=PACK)[:, t, cols]
+            for q in (0, 2, 1, 3):
+                nc.sync.dma_start(weights[t][32 * q : 32 * q + 32, cols], rows)
+
         nc.sync.dma_start(wg_raw_w[:], wg_words.bitcast(I32).rearrange("a p w -> p a w"))
+        nc.sync.dma_start(picks[:], offs)
+        load_scales(tab_s, tab_scales)
+        load_words(0)
         load_wv(0)
         load_scales(wg_raw_s, wg_scales)
-        load_words(1)
         load_wv(1)
+        load_words(1)
+        load_weights(0, slice(0, S))
         nc.sync.dma_start(places[:], offs2)
-        for q in quadrants:
-            nc.sync.dma_start(wgs_first[32 * q : 32 * q + 32, :], wgs_rows[:, 0, :])
-        for q in quadrants:
-            nc.sync.dma_start(wgs_rest[32 * q : 32 * q + 32, :, :], wgs_rows[:, 1:, :])
+        load_weights(1, slice(0, S))
         nc.sync.dma_start(wo_raw[:], wo.rearrange("(p j) n -> p j n", j=PACK))
-        base_rows = base.rearrange("(p j) t -> p j t", j=PACK)
-        for c, w in enumerate(CHUNKS):
-            nc.sync.dma_start(base_c[c][:], base_rows[:, :, starts[c] : starts[c] + w])
+        load_weights(2, slice(0, S))
+        nc.sync.dma_start(base_sb[:], base.rearrange("(p j) t -> p j t", j=PACK))
+        load_weights(3, slice(0, S))
 
         key_w = [[held([P, HALF], U32, f"key_w{a}_{s}") for s in range(2)] for a in range(PASSES)]
         key_s = [[held([P, HALF], U8, f"key_s{a}_{s}") for s in range(2)] for a in range(PASSES)]
@@ -112,11 +112,13 @@ def tile_list_landmark_gated_damping_kernel(
         wg_w = held([P, PASSES, H], U16, "wg_w")
         wg_s = held([P, PASSES, H], U8, "wg_s")
 
-        def permute_wg():
+        def permute_wg_words():
             nc.vector.tensor_copy(
                 wg_w[:].rearrange("p a (t m) -> p a t m", t=PACK),
                 wg_raw_w[:].bitcast(U16).rearrange("p a (m t) -> p a t m", t=PACK),
             )
+
+        def permute_wg_scales():
             nc.vector.tensor_copy(
                 wg_s[:].rearrange("p a (t m) -> p a t m", t=PACK),
                 wg_raw_s[:].bitcast(U8).rearrange("p a (m t) -> p a t m", t=PACK),
@@ -126,22 +128,23 @@ def tile_list_landmark_gated_damping_kernel(
         wv_w = [held([P, H], U32, f"wv_w{a}") for a in range(PASSES)]
         wv_s = [held([P, H], U8, f"wv_s{a}") for a in range(PASSES)]
 
-        def round_wv(a, t0, t1):
+        def round_wv(a):
             nc.scalar.activation(
-                wv_bf[a][:, t0:t1, :, :].rearrange("p t m j -> p m j t"),
-                wv_raw[a][:].rearrange("p j (m t) -> p m j t", t=PACK)[:, :, :, t0:t1],
+                wv_bf[a][:].rearrange("p t m j -> p m j t"),
+                wv_raw[a][:].rearrange("p j (m t) -> p m j t", t=PACK),
                 ACT.Copy,
             )
 
-        def quantize_wv(a, t0, t1):
-            cols = slice(t0 * P, t1 * P)
+        def quantize_wv(a):
             nc.vector.quantize_mx(
-                out=wv_w[a][:, cols].bitcast(FP8X4),
-                scales=wv_s[a][:, cols],
-                in_=wv_bf[a][:, t0:t1, :, :].rearrange("p t m j -> p (t m j)"),
+                out=wv_w[a][:].bitcast(FP8X4),
+                scales=wv_s[a][:],
+                in_=wv_bf[a][:].rearrange("p t m j -> p (t m j)"),
             )
 
         gated = [held([P, S], F32, f"gated{t}") for t in range(PACK)]
+
+        values = [stage.tile([P, S], F32, name="result") for t in range(PACK)]
 
         def gate(t, s):
             cols = slice(t * P, (t + 1) * P)
@@ -158,6 +161,10 @@ def tile_list_landmark_gated_damping_kernel(
                 )
             nc.scalar.activation(gated[t][:, s * HALF : (s + 1) * HALF], acc[:], ACT.Sigmoid)
 
+        def weigh(t, s0, s1):
+            cols = slice(s0 * HALF, s1 * HALF)
+            nc.gpsimd.tensor_tensor(gated[t][:, cols], gated[t][:, cols], weights[t][:, cols], MULT)
+
         def value(t, s):
             cols = slice(t * P, (t + 1) * P)
             acc = psum.tile([P, BANK], F32, name="acc")
@@ -172,49 +179,56 @@ def tile_list_landmark_gated_damping_kernel(
                     stop=(a == PASSES - 1),
                 )
             half = gated[t][:, s * HALF : (s + 1) * HALF]
-            nc.vector.tensor_tensor(half, acc[:], half, MULT)
+            if (t, s) == (0, 0):
+                first = values[t][:, 0:HALF]
+                nc.vector.tensor_tensor(first, acc[:], weights[t][:, 0:HALF], MULT)
+                nc.vector.tensor_tensor(half, half, first, MULT)
+            else:
+                nc.scalar.copy(values[t][:, s * HALF : (s + 1) * HALF], acc[:])
+
+        def combine(t, s0, s1):
+            cols = slice(s0 * HALF, s1 * HALF)
+            weigh(t, s0, s1)
+            nc.gpsimd.tensor_tensor(gated[t][:, cols], gated[t][:, cols], values[t][:, cols], MULT)
 
         def scatter(t, s0, s1):
             cols = slice(s0 * HALF, s1 * HALF)
-            weights = wgs_first[:, cols] if t == 0 else wgs_rest[:, t - 1, cols]
             offsets = places[:, s0 * HALF // 16 : s1 * HALF // 16]
-            nc.vector.tensor_tensor(pages[t % 2][:].indirect(offsets), gated[t][:, cols], weights, MULT)
+            nc.vector.tensor_copy(pages[t % 2][:].indirect(offsets), gated[t][:, cols])
 
-        def damp(t, c):
-            factor = damp_c[c][:, t, :]
-            nc.scalar.activation(factor, pages[t % 2][:, starts[c] : starts[c] + CHUNKS[c]], ACT.Square)
-            nc.scalar.activation(factor, factor, ACT.Abs_reciprocal_sqrt, bias=1.0)
+        def damp(t, cols):
+            factor = factors[:, t, cols]
+            squares = ring.tile([P, cols.stop - cols.start], F32, name="squares")
+            nc.scalar.activation(squares[:], pages[t % 2][:, cols], ACT.Square)
+            nc.scalar.activation(factor, squares[:], ACT.Abs_reciprocal_sqrt, bias=1.0)
 
-        round_wv(0, 0, PACK)
-        round_wv(1, 0, 1)
-        round_wv(1, 1, PACK)
+        round_wv(0)
+        round_wv(1)
+        permute_wg_words()
+        for s in range(2):
+            for a in range(PASSES):
+                gather_scales(a, s)
         gather_words(0, 0)
-        gather_scales(0, 0)
-        gather_scales(1, 0)
-        permute_wg()
-        quantize_wv(0, 0, PACK)
-        gather_words(1, 0)
-        quantize_wv(1, 0, 1)
-        gate(0, 0)
         gather_words(0, 1)
-        gather_scales(0, 1)
-        gather_scales(1, 1)
+        permute_wg_scales()
+        quantize_wv(0)
+        quantize_wv(1)
+        gather_words(1, 0)
+        gate(0, 0)
         gather_words(1, 1)
         value(0, 0)
         gate(0, 1)
-        quantize_wv(1, 1, 2)
-        quantize_wv(1, 2, PACK)
-        scatter(0, 0, 1)
         value(0, 1)
+        scatter(0, 0, 1)
+        combine(0, 1, 2)
         for t in range(1, PACK):
-            gate(t, 0)
-            gate(t, 1)
-        value(1, 0)
+            for s in range(2):
+                gate(t, s)
+                value(t, s)
         scatter(0, 1, 2)
-        value(1, 1)
 
         wo_bf = held([P, N, PACK], BF16, "wo_bf")
-        wo_w = held([P, N], U32, "wo_w")
+        wo_w = held([P, N], U32, f"gated{PACK - 1}")
         wo_s = held([P, N], U8, "wo_s")
         nc.scalar.activation(
             wo_bf[:].rearrange("p (c i) j -> p c j i", i=4),
@@ -223,12 +237,11 @@ def tile_list_landmark_gated_damping_kernel(
         )
 
         for t in range(1, PACK):
-            for c in range(len(CHUNKS)):
-                damp(t - 1, c)
-            if t + 1 < PACK:
-                value(t + 1, 0)
-                value(t + 1, 1)
-            scatter(t, 0, 2)
+            damp(t - 1, slice(0, T2 // 2))
+            damp(t - 1, slice(T2 // 2, T2))
+            for s0, s1 in ((0, 1), (1, 2)) if t == 1 else ((0, 2),):
+                combine(t, s0, s1)
+                scatter(t, s0, s1)
 
         for n0, n1 in ((0, 512), (512, N)):
             nc.vector.quantize_mx(
@@ -241,14 +254,15 @@ def tile_list_landmark_gated_damping_kernel(
 
         def states(c):
             w = CHUNKS[c]
-            damp(PACK - 1, c)
+            cols = slice(starts[c], starts[c] + w)
+            damp(PACK - 1, cols)
             z_bf = ring.tile([P, w, PACK], BF16, name="z_bf", align_bytes=64)
             z_w = ring.tile([P, w], U32, name="z_w", align_bytes=64)
             z_s = ring.tile([P, w], U8, name="z_s", align_bytes=64)
             nc.vector.tensor_tensor(
                 z_bf[:].rearrange("p (c i) j -> p c j i", i=4),
-                base_c[c][:].rearrange("p j (c i) -> p c j i", i=4),
-                damp_c[c][:].rearrange("p j (c i) -> p c j i", i=4),
+                base_sb[:, :, cols].rearrange("p j (c i) -> p c j i", i=4),
+                factors[:, :, cols].rearrange("p j (c i) -> p c j i", i=4),
                 MULT,
             )
             nc.vector.quantize_mx(
@@ -259,29 +273,33 @@ def tile_list_landmark_gated_damping_kernel(
         def project(c, z_w, z_s):
             w = CHUNKS[c]
             per_bank = BANK // w
-            banks = N // P // per_bank
-            for n0 in range(0, N // P, 2):
-                result = stage.tile([P, 2, w], F32, name="result")
-                for n1 in range(n0, n0 + 2, per_bank):
-                    acc = psum.tile([P, per_bank, w], F32, name="acc")
-                    for i in range(per_bank):
-                        cols = slice((n1 + i) * P, (n1 + i + 1) * P)
+            per_store = max(2, per_bank)
+            firsts = list(range(0, N // P, per_bank))
+            for n0 in range(0, N // P, per_store):
+                n_end = min(n0 + per_store, N // P)
+                result = stage.tile([P, n_end - n0, w], F32, name="result")
+                for n1 in range(n0, n_end, per_bank):
+                    count = min(per_bank, n_end - n1)
+                    acc = psum.tile([P, count, w], F32, name="acc")
+                    for i in range(count):
+                        rows = slice((n1 + i) * P, (n1 + i + 1) * P)
                         nc.tensor.matmul_mx(
                             out=acc[:, i, :],
-                            lhsT=wo_w[:, cols].bitcast(FP8X4),
-                            lhsT_scale=wo_s[:, cols],
+                            lhsT=wo_w[:, rows].bitcast(FP8X4),
+                            lhsT_scale=wo_s[:, rows],
                             rhs=z_w[:].bitcast(FP8X4),
                             rhs_scale=z_s[:],
                             start=True,
                             stop=True,
                         )
-                    part = result[:, n1 - n0 : n1 - n0 + per_bank, :]
-                    bank = n1 // per_bank
-                    if (bank + 1) * VECTOR_BANKS[c] // banks > bank * VECTOR_BANKS[c] // banks:
+                    part = result[:, n1 - n0 : n1 - n0 + count, :]
+                    bank = firsts.index(n1)
+                    share = VECTOR_BANKS[c]
+                    if (bank + 1) * share // len(firsts) > bank * share // len(firsts):
                         nc.vector.tensor_copy(part, acc[:])
                     else:
                         nc.scalar.copy(part, acc[:])
-                nc.sync.dma_start(out_rows[:, n0 : n0 + 2, starts[c] : starts[c] + w], result[:])
+                nc.sync.dma_start(out_rows[:, n0:n_end, starts[c] : starts[c] + w], result[:])
 
         made = states(0)
         for c in range(len(CHUNKS)):

@@ -15,14 +15,15 @@ FP8X4 = mybir.dt.float8_e4m3fn_x4
 FP4X4 = mybir.dt.float4_e2m1fn_x4
 ACT = mybir.ActivationFunctionType
 MULT = mybir.AluOpType.mult
+ADD = mybir.AluOpType.add
 
 P = 128
 PACK = 4
 PASSES = K // (P * PACK)
 HALF = S // 2
 BANK = 512
-CHUNKS = (128, 128, 256, 512, 512, 256, 256)
-VECTOR_BANKS = (0, 0, 0, 1, 2, 1, 2)
+CHUNKS = (128, 128, 256, 512, 512, 512)
+VECTOR_BANKS = (0, 0, 0, 1, 1, 3)
 
 
 def tile_list_landmark_gated_damping_kernel(
@@ -33,7 +34,7 @@ def tile_list_landmark_gated_damping_kernel(
         lists = ctx.enter_context(tc.tile_pool(name="lists", bufs=1))
         keep = ctx.enter_context(tc.tile_pool(name="keep", bufs=1))
         ring = ctx.enter_context(tc.tile_pool(name="ring", bufs=2))
-        stage = ctx.enter_context(tc.tile_pool(name="stage", bufs=5))
+        stage = ctx.enter_context(tc.tile_pool(name="stage", bufs=7))
         psum = ctx.enter_context(tc.psum_pool(name="psum", bufs=8))
 
         def held(shape, dtype, name):
@@ -52,15 +53,14 @@ def tile_list_landmark_gated_damping_kernel(
         starts = [sum(CHUNKS[:c]) for c in range(len(CHUNKS))]
         base_sb = held([P, PACK, T2], F32, "base_sb")
         factors = held([P, PACK, T2], F32, "factors")
-        pages = [held([P, T2], F32, f"page{i}") for i in range(2)]
         warm = held([P, 2], F32, "warm")
 
-        nc.vector.memset(tab_s[:], 0)
-        nc.vector.memset(wg_raw_s[:], 0)
+        nc.gpsimd.memset(tab_s[:], 0)
+        nc.gpsimd.memset(wg_raw_s[:], 0)
+        odd_page = held([P, T2], F32, "odd_page")
+        nc.gpsimd.memset(odd_page[:], 0.0)
         nc.vector.memset(warm[:, 0:1], 0.0)
         nc.scalar.activation(warm[:, 1:2], warm[:, 0:1], ACT.Sigmoid)
-        for page in pages:
-            nc.vector.memset(page[:], 0.0)
 
         def load_words(a):
             nc.sync.dma_start(tab_w[a][:], tab_words[a].rearrange("p t i -> p (t i)").bitcast(I32))
@@ -89,13 +89,17 @@ def tile_list_landmark_gated_damping_kernel(
         load_scales(wg_raw_s, wg_scales)
         load_wv(1)
         load_words(1)
-        load_weights(0, slice(0, S))
+        load_weights(0, slice(0, HALF))
         nc.sync.dma_start(places[:], offs2)
-        load_weights(1, slice(0, S))
+        load_weights(1, slice(0, HALF))
+        load_weights(0, slice(HALF, S))
+        load_weights(1, slice(HALF, S))
         nc.sync.dma_start(wo_raw[:], wo.rearrange("(p j) n -> p j n", j=PACK))
         load_weights(2, slice(0, S))
-        nc.sync.dma_start(base_sb[:], base.rearrange("(p j) t -> p j t", j=PACK))
         load_weights(3, slice(0, S))
+        base_rows = base.rearrange("(p j) t -> p j t", j=PACK)
+        for cols in (slice(0, T2 // 2), slice(T2 // 2, T2)):
+            nc.sync.dma_start(base_sb[:, :, cols], base_rows[:, :, cols])
 
         key_w = [[held([P, HALF], U32, f"key_w{a}_{s}") for s in range(2)] for a in range(PASSES)]
         key_s = [[held([P, HALF], U8, f"key_s{a}_{s}") for s in range(2)] for a in range(PASSES)]
@@ -119,7 +123,7 @@ def tile_list_landmark_gated_damping_kernel(
             )
 
         def permute_wg_scales():
-            nc.vector.tensor_copy(
+            nc.gpsimd.tensor_copy(
                 wg_s[:].rearrange("p a (t m) -> p a t m", t=PACK),
                 wg_raw_s[:].bitcast(U8).rearrange("p a (m t) -> p a t m", t=PACK),
             )
@@ -144,7 +148,8 @@ def tile_list_landmark_gated_damping_kernel(
 
         gated = [held([P, S], F32, f"gated{t}") for t in range(PACK)]
 
-        values = [stage.tile([P, S], F32, name="result") for t in range(PACK)]
+        values = [stage.tile([P, S], F32, name="result") for t in range(PACK - 1)]
+        values.append(held([P, S], F32, "last_values"))
 
         def gate(t, s):
             cols = slice(t * P, (t + 1) * P)
@@ -202,9 +207,16 @@ def tile_list_landmark_gated_damping_kernel(
             nc.scalar.activation(squares[:], pages[t % 2][:, cols], ACT.Square)
             nc.scalar.activation(factor, squares[:], ACT.Abs_reciprocal_sqrt, bias=1.0)
 
+        def damp_plane(t):
+            damp(t, slice(0, T2 // 2))
+            damp(t, slice(T2 // 2, T2))
+
         round_wv(0)
         round_wv(1)
         permute_wg_words()
+        even_page = held([P, T2], F32, "wg_raw_w")
+        nc.gpsimd.memset(even_page[:], 0.0)
+        pages = (even_page, odd_page)
         for s in range(2):
             for a in range(PASSES):
                 gather_scales(a, s)
@@ -217,32 +229,26 @@ def tile_list_landmark_gated_damping_kernel(
         gate(0, 0)
         gather_words(1, 1)
         value(0, 0)
-        gate(0, 1)
-        value(0, 1)
         scatter(0, 0, 1)
-        combine(0, 1, 2)
-        for t in range(1, PACK):
+        for t, s in ((1, 0), (0, 1), (1, 1)):
+            gate(t, s)
+            value(t, s)
+            combine(t, s, s + 1)
+            scatter(t, s, s + 1)
+        for t in range(2, PACK):
             for s in range(2):
                 gate(t, s)
                 value(t, s)
-        scatter(0, 1, 2)
+        for t in range(2, PACK):
+            damp_plane(t - 2)
+            combine(t, 0, 2)
+            scatter(t, 0, 2)
+        damp_plane(2)
 
-        wo_bf = held([P, N, PACK], BF16, "wo_bf")
+        wo_bf = held([P, N, PACK], BF16, "last_values")
         wo_w = held([P, N], U32, f"gated{PACK - 1}")
         wo_s = held([P, N], U8, "wo_s")
-        nc.scalar.activation(
-            wo_bf[:].rearrange("p (c i) j -> p c j i", i=4),
-            wo_raw[:].rearrange("p j (c i) -> p c j i", i=4),
-            ACT.Copy,
-        )
-
-        for t in range(1, PACK):
-            damp(t - 1, slice(0, T2 // 2))
-            damp(t - 1, slice(T2 // 2, T2))
-            for s0, s1 in ((0, 1), (1, 2)) if t == 1 else ((0, 2),):
-                combine(t, s0, s1)
-                scatter(t, s0, s1)
-
+        nc.gpsimd.tensor_scalar(wo_bf[:], wo_raw[:].rearrange("p j n -> p n j"), 1.0, 0.0, MULT, ADD)
         for n0, n1 in ((0, 512), (512, N)):
             nc.vector.quantize_mx(
                 out=wo_w[:, n0:n1].bitcast(FP8X4),
@@ -252,21 +258,26 @@ def tile_list_landmark_gated_damping_kernel(
 
         out_rows = out.rearrange("(n p) t -> p n t", p=P)
 
+        z_halves = [held([P, T2 // 2, PACK], BF16, f"wv_raw{a}") for a in range(PASSES)]
+        z_words = held([P, T2], U32, "wv_bf0")
+        z_scales = held([P, T2], U8, "wv_bf1")
+
         def states(c):
             w = CHUNKS[c]
             cols = slice(starts[c], starts[c] + w)
             damp(PACK - 1, cols)
-            z_bf = ring.tile([P, w, PACK], BF16, name="z_bf", align_bytes=64)
-            z_w = ring.tile([P, w], U32, name="z_w", align_bytes=64)
-            z_s = ring.tile([P, w], U8, name="z_s", align_bytes=64)
+            half, first = divmod(starts[c], T2 // 2)
+            z_bf = z_halves[half][:, first : first + w, :]
+            z_w = z_words[:, cols]
+            z_s = z_scales[:, cols]
             nc.vector.tensor_tensor(
-                z_bf[:].rearrange("p (c i) j -> p c j i", i=4),
+                z_bf.rearrange("p (c i) j -> p c j i", i=4),
                 base_sb[:, :, cols].rearrange("p j (c i) -> p c j i", i=4),
                 factors[:, :, cols].rearrange("p j (c i) -> p c j i", i=4),
                 MULT,
             )
             nc.vector.quantize_mx(
-                out=z_w[:].bitcast(FP8X4), scales=z_s[:], in_=z_bf[:].rearrange("p c j -> p (c j)")
+                out=z_w.bitcast(FP8X4), scales=z_s, in_=z_bf.rearrange("p c j -> p (c j)")
             )
             return z_w, z_s
 
@@ -287,8 +298,8 @@ def tile_list_landmark_gated_damping_kernel(
                             out=acc[:, i, :],
                             lhsT=wo_w[:, rows].bitcast(FP8X4),
                             lhsT_scale=wo_s[:, rows],
-                            rhs=z_w[:].bitcast(FP8X4),
-                            rhs_scale=z_s[:],
+                            rhs=z_w.bitcast(FP8X4),
+                            rhs_scale=z_s,
                             start=True,
                             stop=True,
                         )

@@ -23,6 +23,8 @@ PASSES = K // (P * PACK)
 HALF = S // 2
 BANK = 512
 CHUNKS = (128, 128, 256, 512, 512, 512)
+EARLY = 4
+LAG = 3
 VECTOR_BANKS = (0, 0, 0, 1, 1, 3)
 
 
@@ -32,10 +34,10 @@ def tile_list_landmark_gated_damping_kernel(
     nc = tc.nc
     with ExitStack() as ctx:
         lists = ctx.enter_context(tc.tile_pool(name="lists", bufs=1))
+        shared = ctx.enter_context(tc.tile_pool(name="shared", bufs=1))
         keep = ctx.enter_context(tc.tile_pool(name="keep", bufs=1))
-        ring = ctx.enter_context(tc.tile_pool(name="ring", bufs=2))
         stage = ctx.enter_context(tc.tile_pool(name="stage", bufs=7))
-        psum = ctx.enter_context(tc.psum_pool(name="psum", bufs=8))
+        psum = ctx.enter_context(tc.psum_pool(name="psum", bufs=1))
 
         def held(shape, dtype, name):
             return keep.tile(shape, dtype, name=name, align_bytes=64)
@@ -43,24 +45,31 @@ def tile_list_landmark_gated_damping_kernel(
         picks = lists.tile([P, S // 16], U16, name="picks")
         places = lists.tile([P, S // 16], U16, name="places")
 
-        tab_w = [held([P, T], I32, f"tab_w{a}") for a in range(PASSES)]
-        tab_s = held([P, PASSES, T // 4], I32, "tab_s")
+        def placed(shape, dtype, name, slot):
+            return shared.tile(shape, dtype, name=name, align_bytes=64, offset=slot * T * 4)
+
+        tab_w = [placed([P, T], I32, f"tab_w{a}", a) for a in range(PASSES)]
+        wv_raw = [placed([P, PACK, H], F32, f"wv_raw{a}", PASSES + a) for a in range(PASSES)]
+        tab_rows = held([P, T // 4], I32, "tab_rows")
+        key_s = held([P, PASSES, S // 4], I32, "key_s")
         wg_raw_w = held([P, PASSES, H // 2], I32, "wg_raw_w")
         wg_raw_s = held([P, PASSES, H // 4], I32, "wg_raw_s")
-        wv_raw = [held([P, PACK, H], F32, f"wv_raw{a}") for a in range(PASSES)]
         weights = [held([P, S], F32, f"weights{t}") for t in range(PACK)]
         wo_raw = held([P, PACK, N], F32, "wo_raw")
         starts = [sum(CHUNKS[:c]) for c in range(len(CHUNKS))]
         base_sb = held([P, PACK, T2], F32, "base_sb")
-        factors = held([P, PACK, T2], F32, "factors")
         warm = held([P, 2], F32, "warm")
+        pages = [held([P, T2], F32, f"page{i}") for i in range(2)]
 
-        nc.gpsimd.memset(tab_s[:], 0)
         nc.gpsimd.memset(wg_raw_s[:], 0)
-        odd_page = held([P, T2], F32, "odd_page")
-        nc.gpsimd.memset(odd_page[:], 0.0)
+        nc.gpsimd.memset(tab_rows[32:64, :], 0)
+        nc.gpsimd.memset(tab_rows[64:128, :], 0)
+        nc.gpsimd.memset(key_s[:], 0)
+        nc.gpsimd.memset(pages[0][:], 0.0)
         nc.vector.memset(warm[:, 0:1], 0.0)
         nc.scalar.activation(warm[:, 1:2], warm[:, 0:1], ACT.Sigmoid)
+        nc.vector.memset(pages[1][:, 0 : T2 // 2 + 1], 0.0)
+        nc.vector.memset(pages[1][:, T2 // 2 + 1 : T2], 0.0)
 
         def load_words(a):
             nc.sync.dma_start(tab_w[a][:], tab_words[a].rearrange("p t i -> p (t i)").bitcast(I32))
@@ -81,28 +90,8 @@ def tile_list_landmark_gated_damping_kernel(
             for q in (0, 2, 1, 3):
                 nc.sync.dma_start(weights[t][32 * q : 32 * q + 32, cols], rows)
 
-        nc.sync.dma_start(wg_raw_w[:], wg_words.bitcast(I32).rearrange("a p w -> p a w"))
-        nc.sync.dma_start(picks[:], offs)
-        load_scales(tab_s, tab_scales)
-        load_words(0)
-        load_wv(0)
-        load_scales(wg_raw_s, wg_scales)
-        load_wv(1)
-        load_words(1)
-        load_weights(0, slice(0, HALF))
-        nc.sync.dma_start(places[:], offs2)
-        load_weights(1, slice(0, HALF))
-        load_weights(0, slice(HALF, S))
-        load_weights(1, slice(HALF, S))
-        nc.sync.dma_start(wo_raw[:], wo.rearrange("(p j) n -> p j n", j=PACK))
-        load_weights(2, slice(0, S))
-        load_weights(3, slice(0, S))
-        base_rows = base.rearrange("(p j) t -> p j t", j=PACK)
-        for cols in (slice(0, T2 // 2), slice(T2 // 2, T2)):
-            nc.sync.dma_start(base_sb[:, :, cols], base_rows[:, :, cols])
-
         key_w = [[held([P, HALF], U32, f"key_w{a}_{s}") for s in range(2)] for a in range(PASSES)]
-        key_s = [[held([P, HALF], U8, f"key_s{a}_{s}") for s in range(2)] for a in range(PASSES)]
+        picked_rows = held([P, S], U8, "picked_rows")
 
         def half_of(offsets, s):
             return offsets[:, s * HALF // 16 : (s + 1) * HALF // 16]
@@ -110,8 +99,36 @@ def tile_list_landmark_gated_damping_kernel(
         def gather_words(a, s):
             nc.vector.tensor_copy(key_w[a][s][:], tab_w[a][:].bitcast(U32).indirect(half_of(picks, s)))
 
-        def gather_scales(a, s):
-            nc.vector.tensor_copy(key_s[a][s][:], tab_s[:, a, :].bitcast(U8).indirect(half_of(picks, s)))
+        def gather_scales():
+            nc.vector.tensor_copy(picked_rows[:], tab_rows[:].bitcast(U8).indirect(picks[:]))
+            for q in (0, 2, 1, 3):
+                nc.sync.dma_start(
+                    key_s[32 * q : 32 * q + 4, :, :], picked_rows[:].bitcast(I32)[8 * q : 8 * q + 8, :]
+                )
+
+        def key_scales(a, s):
+            return key_s[:, a, s * HALF // 4 : (s + 1) * HALF // 4].bitcast(U8)
+
+        nc.sync.dma_start(picks[:], offs)
+        nc.sync.dma_start(tab_rows[0:32, :], tab_scales.bitcast(I32).rearrange("a q w -> q a w"))
+        load_scales(wg_raw_s, wg_scales)
+        load_words(0)
+        nc.sync.dma_start(wg_raw_w[:], wg_words.bitcast(I32).rearrange("a p w -> p a w"))
+        load_words(1)
+        gather_scales()
+        load_wv(0)
+        load_wv(1)
+        nc.sync.dma_start(places[:], offs2)
+        load_weights(0, slice(0, HALF))
+        load_weights(1, slice(0, HALF))
+        load_weights(0, slice(HALF, S))
+        load_weights(1, slice(HALF, S))
+        load_weights(2, slice(0, S))
+        load_weights(3, slice(0, S))
+        nc.sync.dma_start(wo_raw[:], wo.rearrange("(p j) n -> p j n", j=PACK))
+        base_rows = base.rearrange("(p j) t -> p j t", j=PACK)
+        for cols in (slice(0, T2 // 2), slice(T2 // 2, T2)):
+            nc.sync.dma_start(base_sb[:, :, cols], base_rows[:, :, cols])
 
         wg_w = held([P, PASSES, H], U16, "wg_w")
         wg_s = held([P, PASSES, H], U8, "wg_s")
@@ -128,22 +145,22 @@ def tile_list_landmark_gated_damping_kernel(
                 wg_raw_s[:].bitcast(U8).rearrange("p a (m t) -> p a t m", t=PACK),
             )
 
-        wv_bf = [held([P, PACK, P, PACK], BF16, f"wv_bf{a}") for a in range(PASSES)]
         wv_w = [held([P, H], U32, f"wv_w{a}") for a in range(PASSES)]
         wv_s = [held([P, H], U8, f"wv_s{a}") for a in range(PASSES)]
 
-        def round_wv(a):
-            nc.scalar.activation(
-                wv_bf[a][:].rearrange("p t m j -> p m j t"),
-                wv_raw[a][:].rearrange("p j (m t) -> p m j t", t=PACK),
-                ACT.Copy,
+        def round_wv(a, t0, t1):
+            rounded = held([P, t1 - t0, P, PACK], BF16, f"wv_bf{a}")
+            nc.vector.tensor_copy(
+                rounded[:].rearrange("p t m j -> p m j t"),
+                wv_raw[a][:].rearrange("p j (m t) -> p m j t", t=PACK)[:, :, :, t0:t1],
             )
+            return rounded
 
-        def quantize_wv(a):
+        def quantize_wv(a, t0, t1, rounded):
             nc.vector.quantize_mx(
-                out=wv_w[a][:].bitcast(FP8X4),
-                scales=wv_s[a][:],
-                in_=wv_bf[a][:].rearrange("p t m j -> p (t m j)"),
+                out=wv_w[a][:, t0 * P : t1 * P].bitcast(FP8X4),
+                scales=wv_s[a][:, t0 * P : t1 * P],
+                in_=rounded[:].rearrange("p t m j -> p (t m j)"),
             )
 
         gated = [held([P, S], F32, f"gated{t}") for t in range(PACK)]
@@ -153,16 +170,17 @@ def tile_list_landmark_gated_damping_kernel(
 
         def gate(t, s):
             cols = slice(t * P, (t + 1) * P)
-            acc = psum.tile([P, BANK], F32, name="acc")
-            for a in range(PASSES):
+            acc = psum.tile([P, BANK], F32, name=f"bank{2 * t + s}")
+            order = (1, 0)
+            for a in order:
                 nc.tensor.matmul_mx(
                     out=acc[:],
                     lhsT=wg_w[:, a, cols].bitcast(FP4X4),
                     lhsT_scale=wg_s[:, a, cols],
                     rhs=key_w[a][s][:].bitcast(FP8X4),
-                    rhs_scale=key_s[a][s][:],
-                    start=(a == 0),
-                    stop=(a == PASSES - 1),
+                    rhs_scale=key_scales(a, s),
+                    start=(a == order[0]),
+                    stop=(a == order[-1]),
                 )
             nc.scalar.activation(gated[t][:, s * HALF : (s + 1) * HALF], acc[:], ACT.Sigmoid)
 
@@ -172,66 +190,59 @@ def tile_list_landmark_gated_damping_kernel(
 
         def value(t, s):
             cols = slice(t * P, (t + 1) * P)
-            acc = psum.tile([P, BANK], F32, name="acc")
-            for a in range(PASSES):
+            acc = psum.tile([P, BANK], F32, name=f"bank{(2 * t + s + 4) % 8}")
+            order = (0, 1) if (t, s) == (0, 0) else (1, 0)
+            for a in order:
                 nc.tensor.matmul_mx(
                     out=acc[:],
                     lhsT=wv_w[a][:, cols].bitcast(FP8X4),
                     lhsT_scale=wv_s[a][:, cols],
                     rhs=key_w[a][s][:].bitcast(FP8X4),
-                    rhs_scale=key_s[a][s][:],
-                    start=(a == 0),
-                    stop=(a == PASSES - 1),
+                    rhs_scale=key_scales(a, s),
+                    start=(a == order[0]),
+                    stop=(a == order[-1]),
                 )
             half = gated[t][:, s * HALF : (s + 1) * HALF]
             if (t, s) == (0, 0):
-                first = values[t][:, 0:HALF]
-                nc.vector.tensor_tensor(first, acc[:], weights[t][:, 0:HALF], MULT)
-                nc.vector.tensor_tensor(half, half, first, MULT)
+                nc.vector.tensor_tensor(half, acc[:], half, MULT)
             else:
                 nc.scalar.copy(values[t][:, s * HALF : (s + 1) * HALF], acc[:])
 
         def combine(t, s0, s1):
-            cols = slice(s0 * HALF, s1 * HALF)
-            weigh(t, s0, s1)
-            nc.gpsimd.tensor_tensor(gated[t][:, cols], gated[t][:, cols], values[t][:, cols], MULT)
+            for s in range(s0, s1):
+                cols = slice(s * HALF, (s + 1) * HALF)
+                weigh(t, s, s + 1)
+                nc.gpsimd.tensor_tensor(gated[t][:, cols], gated[t][:, cols], values[t][:, cols], MULT)
 
         def scatter(t, s0, s1):
             cols = slice(s0 * HALF, s1 * HALF)
             offsets = places[:, s0 * HALF // 16 : s1 * HALF // 16]
             nc.vector.tensor_copy(pages[t % 2][:].indirect(offsets), gated[t][:, cols])
 
-        def damp(t, cols):
-            factor = factors[:, t, cols]
-            squares = ring.tile([P, cols.stop - cols.start], F32, name="squares")
+        factors = placed([P, PACK, T2], F32, "factors", 0)
+
+        def damp(t, cols, name):
+            squares = held([P, cols.stop - cols.start], F32, name)
             nc.scalar.activation(squares[:], pages[t % 2][:, cols], ACT.Square)
-            nc.scalar.activation(factor, squares[:], ACT.Abs_reciprocal_sqrt, bias=1.0)
+            nc.scalar.activation(factors[:, t, cols], squares[:], ACT.Abs_reciprocal_sqrt, bias=1.0)
 
-        def damp_plane(t):
-            damp(t, slice(0, T2 // 2))
-            damp(t, slice(T2 // 2, T2))
-
-        round_wv(0)
-        round_wv(1)
-        permute_wg_words()
-        even_page = held([P, T2], F32, "wg_raw_w")
-        nc.gpsimd.memset(even_page[:], 0.0)
-        pages = (even_page, odd_page)
-        for s in range(2):
-            for a in range(PASSES):
-                gather_scales(a, s)
         gather_words(0, 0)
         gather_words(0, 1)
         permute_wg_scales()
-        quantize_wv(0)
-        quantize_wv(1)
+        permute_wg_words()
         gather_words(1, 0)
-        gate(0, 0)
         gather_words(1, 1)
+        for s in range(2):
+            for t in range(2):
+                gate(t, s)
+        quantize_wv(0, 0, PACK, round_wv(0, 0, PACK))
+        quantize_wv(1, 0, 2, round_wv(1, 0, 2))
+        late = round_wv(1, 2, PACK)
+        weigh(0, 0, 1)
         value(0, 0)
+        quantize_wv(1, 2, PACK, late)
         scatter(0, 0, 1)
         for t, s in ((1, 0), (0, 1), (1, 1)):
-            gate(t, s)
             value(t, s)
             combine(t, s, s + 1)
             scatter(t, s, s + 1)
@@ -240,10 +251,10 @@ def tile_list_landmark_gated_damping_kernel(
                 gate(t, s)
                 value(t, s)
         for t in range(2, PACK):
-            damp_plane(t - 2)
+            damp(t - 2, slice(0, T2), "squares")
             combine(t, 0, 2)
             scatter(t, 0, 2)
-        damp_plane(2)
+        damp(2, slice(0, T2), "squares")
 
         wo_bf = held([P, N, PACK], BF16, "last_values")
         wo_w = held([P, N], U32, f"gated{PACK - 1}")
@@ -258,16 +269,17 @@ def tile_list_landmark_gated_damping_kernel(
 
         out_rows = out.rearrange("(n p) t -> p n t", p=P)
 
-        z_halves = [held([P, T2 // 2, PACK], BF16, f"wv_raw{a}") for a in range(PASSES)]
-        z_words = held([P, T2], U32, "wv_bf0")
-        z_scales = held([P, T2], U8, "wv_bf1")
+        z_words = held([P, T2], U32, "squares")
+        z_scales = held([P, T2], U8, "tab_rows")
+        rooms = ["room0", "room1", "room2", "weights0", "weights1", "weights2"]
+
+        def chunk(c):
+            return slice(starts[c], starts[c] + CHUNKS[c])
 
         def states(c):
-            w = CHUNKS[c]
-            cols = slice(starts[c], starts[c] + w)
-            damp(PACK - 1, cols)
-            half, first = divmod(starts[c], T2 // 2)
-            z_bf = z_halves[half][:, first : first + w, :]
+            cols = chunk(c)
+            z_tile = held([P, CHUNKS[c], PACK], BF16, rooms[c])
+            z_bf = z_tile[:]
             z_w = z_words[:, cols]
             z_s = z_scales[:, cols]
             nc.vector.tensor_tensor(
@@ -281,6 +293,8 @@ def tile_list_landmark_gated_damping_kernel(
             )
             return z_w, z_s
 
+        used = []
+
         def project(c, z_w, z_s):
             w = CHUNKS[c]
             per_bank = BANK // w
@@ -291,7 +305,8 @@ def tile_list_landmark_gated_damping_kernel(
                 result = stage.tile([P, n_end - n0, w], F32, name="result")
                 for n1 in range(n0, n_end, per_bank):
                     count = min(per_bank, n_end - n1)
-                    acc = psum.tile([P, count, w], F32, name="acc")
+                    acc = psum.tile([P, count, w], F32, name=f"bank{len(used) % 8}")
+                    used.append(n1)
                     for i in range(count):
                         rows = slice((n1 + i) * P, (n1 + i + 1) * P)
                         nc.tensor.matmul_mx(
@@ -312,8 +327,9 @@ def tile_list_landmark_gated_damping_kernel(
                         nc.scalar.copy(part, acc[:])
                 nc.sync.dma_start(out_rows[:, n0:n_end, starts[c] : starts[c] + w], result[:])
 
-        made = states(0)
+        for c in range(EARLY):
+            damp(PACK - 1, chunk(c), f"early_squares{c % 2}")
         for c in range(len(CHUNKS)):
-            ahead = states(c + 1) if c + 1 < len(CHUNKS) else None
-            project(c, *made)
-            made = ahead
+            project(c, *states(c))
+            if EARLY <= c + LAG < len(CHUNKS):
+                damp(PACK - 1, chunk(c + LAG), rooms[c])

@@ -283,9 +283,9 @@ def tile_list_landmark_gated_damping_kernel(
             z_w = z_words[:, cols]
             z_s = z_scales[:, cols]
             nc.vector.tensor_tensor(
-                z_bf.rearrange("p (c i) j -> p c j i", i=4),
-                base_sb[:, :, cols].rearrange("p j (c i) -> p c j i", i=4),
-                factors[:, :, cols].rearrange("p j (c i) -> p c j i", i=4),
+                z_bf.rearrange("p (c i) j -> p c j i", i=2),
+                base_sb[:, :, cols].rearrange("p j (c i) -> p c j i", i=2),
+                factors[:, :, cols].rearrange("p j (c i) -> p c j i", i=2),
                 MULT,
             )
             nc.vector.quantize_mx(

@@ -15,7 +15,6 @@ FP8X4 = mybir.dt.float8_e4m3fn_x4
 FP4X4 = mybir.dt.float4_e2m1fn_x4
 ACT = mybir.ActivationFunctionType
 MULT = mybir.AluOpType.mult
-ADD = mybir.AluOpType.add
 
 P = 128
 PACK = 4
@@ -26,6 +25,9 @@ CHUNKS = (128, 128, 256, 512, 512, 512)
 EARLY = 4
 LAG = 3
 VECTOR_BANKS = (0, 0, 0, 1, 1, 3)
+STAGES = 12
+GATE_BANKS = ((0, 3), (1, 0), (2, 1), (3, 0))
+VALUE_BANKS = ((2, 0), (3, 1), (4, 5), (6, 7))
 
 
 def tile_list_landmark_gated_damping_kernel(
@@ -36,7 +38,7 @@ def tile_list_landmark_gated_damping_kernel(
         lists = ctx.enter_context(tc.tile_pool(name="lists", bufs=1))
         shared = ctx.enter_context(tc.tile_pool(name="shared", bufs=1))
         keep = ctx.enter_context(tc.tile_pool(name="keep", bufs=1))
-        stage = ctx.enter_context(tc.tile_pool(name="stage", bufs=7))
+        stage = ctx.enter_context(tc.tile_pool(name="stage", bufs=1))
         psum = ctx.enter_context(tc.psum_pool(name="psum", bufs=1))
 
         def held(shape, dtype, name):
@@ -85,10 +87,16 @@ def tile_list_landmark_gated_damping_kernel(
                     scales.bitcast(I32)[:, 4 * q : 4 * q + 4, :].rearrange("a r w -> r a w"),
                 )
 
+        first_weights = held([P, HALF], F32, "first_weights")
+
         def load_weights(t, cols):
-            rows = wgs.rearrange("(m t) j -> m t j", t=PACK)[:, t, cols]
+            tile = first_weights if (t, cols.stop) == (0, HALF) else weights[t]
+            rows = wgs.rearrange("(u t e) j -> t u e j", t=PACK, e=2)[t, :, :, cols]
             for q in (0, 2, 1, 3):
-                nc.sync.dma_start(weights[t][32 * q : 32 * q + 32, cols], rows)
+                nc.sync.dma_start(tile[32 * q : 32 * q + 32, cols], rows)
+
+        def load_plane(tile, source, t):
+            nc.sync.dma_start(tile[:, t, :], source.rearrange("(u t e) c -> t u e c", t=PACK, e=2)[t])
 
         key_w = [[held([P, HALF], U32, f"key_w{a}_{s}") for s in range(2)] for a in range(PASSES)]
         picked_rows = held([P, S], U8, "picked_rows")
@@ -121,38 +129,39 @@ def tile_list_landmark_gated_damping_kernel(
         nc.sync.dma_start(places[:], offs2)
         load_weights(0, slice(0, HALF))
         load_weights(1, slice(0, HALF))
+        for t in range(PACK):
+            load_plane(wo_raw, wo, t)
         load_weights(0, slice(HALF, S))
         load_weights(1, slice(HALF, S))
         load_weights(2, slice(0, S))
+        for t in range(PACK - 1):
+            load_plane(base_sb, base, t)
         load_weights(3, slice(0, S))
-        nc.sync.dma_start(wo_raw[:], wo.rearrange("(p j) n -> p j n", j=PACK))
-        base_rows = base.rearrange("(p j) t -> p j t", j=PACK)
-        for cols in (slice(0, T2 // 2), slice(T2 // 2, T2)):
-            nc.sync.dma_start(base_sb[:, :, cols], base_rows[:, :, cols])
+        load_plane(base_sb, base, PACK - 1)
 
-        wg_w = held([P, PASSES, H], U16, "wg_w")
+        wg_w = held([P, PASSES, H // 2], I32, "wg_w")
         wg_s = held([P, PASSES, H], U8, "wg_s")
 
         def permute_wg_words():
-            nc.vector.tensor_copy(
-                wg_w[:].rearrange("p a (t m) -> p a t m", t=PACK),
-                wg_raw_w[:].bitcast(U16).rearrange("p a (m t) -> p a t m", t=PACK),
+            nc.gpsimd.tensor_copy(
+                wg_w[:].rearrange("p a (t u) -> p a t u", t=PACK),
+                wg_raw_w[:].rearrange("p a (u t) -> p a t u", t=PACK),
             )
 
         def permute_wg_scales():
             nc.gpsimd.tensor_copy(
-                wg_s[:].rearrange("p a (t m) -> p a t m", t=PACK),
-                wg_raw_s[:].bitcast(U8).rearrange("p a (m t) -> p a t m", t=PACK),
+                wg_s[:].rearrange("p a (t u e) -> p a t u e", t=PACK, e=2),
+                wg_raw_s[:].bitcast(U8).rearrange("p a (u t e) -> p a t u e", t=PACK, e=2),
             )
 
         wv_w = [held([P, H], U32, f"wv_w{a}") for a in range(PASSES)]
         wv_s = [held([P, H], U8, f"wv_s{a}") for a in range(PASSES)]
 
-        def round_wv(a, t0, t1):
-            rounded = held([P, t1 - t0, P, PACK], BF16, f"wv_bf{a}")
-            nc.vector.tensor_copy(
-                rounded[:].rearrange("p t m j -> p m j t"),
-                wv_raw[a][:].rearrange("p j (m t) -> p m j t", t=PACK)[:, :, :, t0:t1],
+        def round_wv(a, t0, t1, copy):
+            rounded = held([P, t1 - t0, P, PACK], BF16, f"wv_bf{a}_{t0}")
+            copy(
+                rounded[:].rearrange("p t (u e) j -> p u t j e", e=2),
+                wv_raw[a][:].rearrange("p j (u t e) -> p u t j e", t=PACK, e=2)[:, :, t0:t1, :, :],
             )
             return rounded
 
@@ -165,17 +174,16 @@ def tile_list_landmark_gated_damping_kernel(
 
         gated = [held([P, S], F32, f"gated{t}") for t in range(PACK)]
 
-        values = [stage.tile([P, S], F32, name="result") for t in range(PACK - 1)]
-        values.append(held([P, S], F32, "last_values"))
+        values = [stage.tile([P, S], F32, name=f"values{t}", offset=t * S * 4) for t in range(PACK)]
 
         def gate(t, s):
             cols = slice(t * P, (t + 1) * P)
-            acc = psum.tile([P, BANK], F32, name=f"bank{2 * t + s}")
+            acc = psum.tile([P, BANK], F32, name=f"bank{GATE_BANKS[t][s]}")
             order = (1, 0)
             for a in order:
                 nc.tensor.matmul_mx(
                     out=acc[:],
-                    lhsT=wg_w[:, a, cols].bitcast(FP4X4),
+                    lhsT=wg_w[:, a, t * P // 2 : (t + 1) * P // 2].bitcast(FP4X4),
                     lhsT_scale=wg_s[:, a, cols],
                     rhs=key_w[a][s][:].bitcast(FP8X4),
                     rhs_scale=key_scales(a, s),
@@ -184,13 +192,9 @@ def tile_list_landmark_gated_damping_kernel(
                 )
             nc.scalar.activation(gated[t][:, s * HALF : (s + 1) * HALF], acc[:], ACT.Sigmoid)
 
-        def weigh(t, s0, s1):
-            cols = slice(s0 * HALF, s1 * HALF)
-            nc.gpsimd.tensor_tensor(gated[t][:, cols], gated[t][:, cols], weights[t][:, cols], MULT)
-
         def value(t, s):
             cols = slice(t * P, (t + 1) * P)
-            acc = psum.tile([P, BANK], F32, name=f"bank{(2 * t + s + 4) % 8}")
+            acc = psum.tile([P, BANK], F32, name=f"bank{VALUE_BANKS[t][s]}")
             order = (0, 1) if (t, s) == (0, 0) else (1, 0)
             for a in order:
                 nc.tensor.matmul_mx(
@@ -211,8 +215,11 @@ def tile_list_landmark_gated_damping_kernel(
         def combine(t, s0, s1):
             for s in range(s0, s1):
                 cols = slice(s * HALF, (s + 1) * HALF)
-                weigh(t, s, s + 1)
-                nc.gpsimd.tensor_tensor(gated[t][:, cols], gated[t][:, cols], values[t][:, cols], MULT)
+                weighed = gated[t][:, cols]
+                if (t, s) == (1, 0):
+                    weighed = held([P, HALF], F32, "first_weights")[:]
+                nc.gpsimd.tensor_tensor(weighed, gated[t][:, cols], weights[t][:, cols], MULT)
+                nc.gpsimd.tensor_tensor(gated[t][:, cols], weighed, values[t][:, cols], MULT)
 
         def scatter(t, s0, s1):
             cols = slice(s0 * HALF, s1 * HALF)
@@ -232,34 +239,39 @@ def tile_list_landmark_gated_damping_kernel(
         permute_wg_words()
         gather_words(1, 0)
         gather_words(1, 1)
-        for s in range(2):
-            for t in range(2):
-                gate(t, s)
-        quantize_wv(0, 0, PACK, round_wv(0, 0, PACK))
-        quantize_wv(1, 0, 2, round_wv(1, 0, 2))
-        late = round_wv(1, 2, PACK)
-        weigh(0, 0, 1)
+        gate(0, 0)
+        gate(1, 0)
+        quantize_wv(0, 0, PACK, round_wv(0, 0, PACK, nc.vector.tensor_copy))
+        quantize_wv(1, 0, 2, round_wv(1, 0, 2, nc.vector.tensor_copy))
+        quantize_wv(1, 2, PACK, round_wv(1, 2, PACK, nc.scalar.copy))
+        nc.vector.tensor_tensor(gated[0][:, 0:HALF], gated[0][:, 0:HALF], first_weights[:], MULT)
         value(0, 0)
-        quantize_wv(1, 2, PACK, late)
         scatter(0, 0, 1)
         for t, s in ((1, 0), (0, 1), (1, 1)):
             value(t, s)
+        gate(0, 1)
+        gate(1, 1)
+        for t, s in ((1, 0), (0, 1), (1, 1)):
             combine(t, s, s + 1)
             scatter(t, s, s + 1)
         for t in range(2, PACK):
             for s in range(2):
                 gate(t, s)
                 value(t, s)
+        wo_bf = held([P, N, PACK], BF16, "wo_bf")
+        nc.scalar.activation(
+            wo_bf[:].rearrange("p (c i) j -> p c j i", i=2),
+            wo_raw[:].rearrange("p j (c i) -> p c j i", i=2),
+            ACT.Copy,
+        )
         for t in range(2, PACK):
             damp(t - 2, slice(0, T2), "squares")
             combine(t, 0, 2)
             scatter(t, 0, 2)
         damp(2, slice(0, T2), "squares")
 
-        wo_bf = held([P, N, PACK], BF16, "last_values")
         wo_w = held([P, N], U32, f"gated{PACK - 1}")
         wo_s = held([P, N], U8, "wo_s")
-        nc.gpsimd.tensor_scalar(wo_bf[:], wo_raw[:].rearrange("p j n -> p n j"), 1.0, 0.0, MULT, ADD)
         for n0, n1 in ((0, 512), (512, N)):
             nc.vector.quantize_mx(
                 out=wo_w[:, n0:n1].bitcast(FP8X4),
@@ -271,7 +283,7 @@ def tile_list_landmark_gated_damping_kernel(
 
         z_words = held([P, T2], U32, "squares")
         z_scales = held([P, T2], U8, "tab_rows")
-        rooms = ["room0", "room1", "room2", "weights0", "weights1", "weights2"]
+        rooms = ["room0", "room0", "room2", "weights0", "weights1", "weights2"]
 
         def chunk(c):
             return slice(starts[c], starts[c] + CHUNKS[c])
@@ -280,29 +292,34 @@ def tile_list_landmark_gated_damping_kernel(
             cols = chunk(c)
             z_tile = held([P, CHUNKS[c], PACK], BF16, rooms[c])
             z_bf = z_tile[:]
-            z_w = z_words[:, cols]
-            z_s = z_scales[:, cols]
             nc.vector.tensor_tensor(
                 z_bf.rearrange("p (c i) j -> p c j i", i=2),
                 base_sb[:, :, cols].rearrange("p j (c i) -> p c j i", i=2),
                 factors[:, :, cols].rearrange("p j (c i) -> p c j i", i=2),
                 MULT,
             )
+            return z_bf
+
+        def quantize_states(c, z_bf):
             nc.vector.quantize_mx(
-                out=z_w.bitcast(FP8X4), scales=z_s, in_=z_bf.rearrange("p c j -> p (c j)")
+                out=z_words[:, chunk(c)].bitcast(FP8X4),
+                scales=z_scales[:, chunk(c)],
+                in_=z_bf.rearrange("p c j -> p (c j)"),
             )
-            return z_w, z_s
 
         used = []
 
-        def project(c, z_w, z_s):
+        def project(c):
+            z_w = z_words[:, chunk(c)]
+            z_s = z_scales[:, chunk(c)]
             w = CHUNKS[c]
-            per_bank = BANK // w
-            per_store = max(2, per_bank)
+            per_bank = 2 if w < BANK else 1
+            per_store = per_bank
             firsts = list(range(0, N // P, per_bank))
             for n0 in range(0, N // P, per_store):
                 n_end = min(n0 + per_store, N // P)
-                result = stage.tile([P, n_end - n0, w], F32, name="result")
+                slot = len(used) % STAGES
+                result = stage.tile([P, n_end - n0, w], F32, name=f"result{slot}", offset=slot * BANK * 4)
                 for n1 in range(n0, n_end, per_bank):
                     count = min(per_bank, n_end - n1)
                     acc = psum.tile([P, count, w], F32, name=f"bank{len(used) % 8}")
@@ -321,7 +338,7 @@ def tile_list_landmark_gated_damping_kernel(
                     part = result[:, n1 - n0 : n1 - n0 + count, :]
                     bank = firsts.index(n1)
                     share = VECTOR_BANKS[c]
-                    if (bank + 1) * share // len(firsts) > bank * share // len(firsts):
+                    if bank * share % len(firsts) < share:
                         nc.vector.tensor_copy(part, acc[:])
                     else:
                         nc.scalar.copy(part, acc[:])
@@ -329,7 +346,11 @@ def tile_list_landmark_gated_damping_kernel(
 
         for c in range(EARLY):
             damp(PACK - 1, chunk(c), f"early_squares{c % 2}")
+        quantize_states(0, states(0))
         for c in range(len(CHUNKS)):
-            project(c, *states(c))
             if EARLY <= c + LAG < len(CHUNKS):
                 damp(PACK - 1, chunk(c + LAG), rooms[c])
+            ahead = states(c + 1) if c + 1 < len(CHUNKS) else None
+            project(c)
+            if ahead is not None:
+                quantize_states(c + 1, ahead)

@@ -24,8 +24,9 @@ BANK = 512
 CHUNKS = (128, 128, 256, 512, 512, 512)
 EARLY = 4
 LAG = 3
-VECTOR_BANKS = (0, 0, 0, 1, 1, 3)
+VECTOR_BANKS = (0, 0, 1, 1, 1, 3)
 STAGES = 12
+NARROW = 3
 GATE_BANKS = ((0, 3), (1, 0), (2, 1), (3, 0))
 VALUE_BANKS = ((2, 0), (3, 1), (4, 5), (6, 7))
 
@@ -48,7 +49,7 @@ def tile_list_landmark_gated_damping_kernel(
         places = lists.tile([P, S // 16], U16, name="places")
 
         def placed(shape, dtype, name, slot):
-            return shared.tile(shape, dtype, name=name, align_bytes=64, offset=slot * T * 4)
+            return shared.tile(shape, dtype, name=name, align_bytes=64, offset=int(slot * T * 4))
 
         tab_w = [placed([P, T], I32, f"tab_w{a}", a) for a in range(PASSES)]
         wv_raw = [placed([P, PACK, H], F32, f"wv_raw{a}", PASSES + a) for a in range(PASSES)]
@@ -57,7 +58,7 @@ def tile_list_landmark_gated_damping_kernel(
         wg_raw_w = held([P, PASSES, H // 2], I32, "wg_raw_w")
         wg_raw_s = held([P, PASSES, H // 4], I32, "wg_raw_s")
         weights = [held([P, S], F32, f"weights{t}") for t in range(PACK)]
-        wo_raw = held([P, PACK, N], F32, "wo_raw")
+        wo_raw = placed([P, PACK, N], F32, "wo_raw", 2 * PASSES)
         starts = [sum(CHUNKS[:c]) for c in range(len(CHUNKS))]
         base_sb = held([P, PACK, T2], F32, "base_sb")
         warm = held([P, 2], F32, "warm")
@@ -119,9 +120,9 @@ def tile_list_landmark_gated_damping_kernel(
 
         nc.sync.dma_start(picks[:], offs)
         nc.sync.dma_start(tab_rows[0:32, :], tab_scales.bitcast(I32).rearrange("a q w -> q a w"))
-        load_scales(wg_raw_s, wg_scales)
         load_words(0)
         nc.sync.dma_start(wg_raw_w[:], wg_words.bitcast(I32).rearrange("a p w -> p a w"))
+        load_scales(wg_raw_s, wg_scales)
         load_words(1)
         gather_scales()
         load_wv(0)
@@ -129,15 +130,14 @@ def tile_list_landmark_gated_damping_kernel(
         nc.sync.dma_start(places[:], offs2)
         load_weights(0, slice(0, HALF))
         load_weights(1, slice(0, HALF))
-        for t in range(PACK):
-            load_plane(wo_raw, wo, t)
         load_weights(0, slice(HALF, S))
         load_weights(1, slice(HALF, S))
+        for t in range(PACK):
+            load_plane(wo_raw, wo, t)
         load_weights(2, slice(0, S))
-        for t in range(PACK - 1):
-            load_plane(base_sb, base, t)
         load_weights(3, slice(0, S))
-        load_plane(base_sb, base, PACK - 1)
+        for t in range(PACK):
+            load_plane(base_sb, base, t)
 
         wg_w = held([P, PASSES, H // 2], I32, "wg_w")
         wg_s = held([P, PASSES, H], U8, "wg_s")
@@ -228,8 +228,7 @@ def tile_list_landmark_gated_damping_kernel(
 
         factors = placed([P, PACK, T2], F32, "factors", 0)
 
-        def damp(t, cols, name):
-            squares = held([P, cols.stop - cols.start], F32, name)
+        def damp(t, cols, squares):
             nc.scalar.activation(squares[:], pages[t % 2][:, cols], ACT.Square)
             nc.scalar.activation(factors[:, t, cols], squares[:], ACT.Abs_reciprocal_sqrt, bias=1.0)
 
@@ -265,10 +264,15 @@ def tile_list_landmark_gated_damping_kernel(
             ACT.Copy,
         )
         for t in range(2, PACK):
-            damp(t - 2, slice(0, T2), "squares")
+            damp(t - 2, slice(0, T2), placed([P, T2], F32, "squares", 2 * PASSES))
             combine(t, 0, 2)
             scatter(t, 0, 2)
-        damp(2, slice(0, T2), "squares")
+        damp(2, slice(0, T2), placed([P, T2], F32, "squares", 2 * PASSES))
+
+        wide = slice(starts[NARROW], T2)
+        pairs = held([P, 2, T2 - starts[NARROW], 2], BF16, "pairs")
+        for t in range(2):
+            nc.gpsimd.tensor_tensor(pairs[:, 0, :, t], base_sb[:, t, wide], factors[:, t, wide], MULT)
 
         wo_w = held([P, N], U32, f"gated{PACK - 1}")
         wo_s = held([P, N], U8, "wo_s")
@@ -281,7 +285,7 @@ def tile_list_landmark_gated_damping_kernel(
 
         out_rows = out.rearrange("(n p) t -> p n t", p=P)
 
-        z_words = held([P, T2], U32, "squares")
+        z_words = held([P, T2], U32, "z_words")
         z_scales = held([P, T2], U8, "tab_rows")
         rooms = ["room0", "room0", "room2", "weights0", "weights1", "weights2"]
 
@@ -292,6 +296,19 @@ def tile_list_landmark_gated_damping_kernel(
             cols = chunk(c)
             z_tile = held([P, CHUNKS[c], PACK], BF16, rooms[c])
             z_bf = z_tile[:]
+            if c >= NARROW:
+                own = slice(cols.start - wide.start, cols.stop - wide.start)
+                nc.vector.tensor_tensor(
+                    pairs[:, 1, own, :].rearrange("p (c i) j -> p c j i", i=4),
+                    base_sb[:, 2:PACK, cols].rearrange("p j (c i) -> p c j i", i=4),
+                    factors[:, 2:PACK, cols].rearrange("p j (c i) -> p c j i", i=4),
+                    MULT,
+                )
+                nc.vector.tensor_copy(
+                    z_bf.bitcast(I32).rearrange("p (c i) h -> p c h i", i=2),
+                    pairs[:].rearrange("p h c j -> p h (c j)").bitcast(I32)[:, :, own].rearrange("p h (c i) -> p c h i", i=2),
+                )
+                return z_bf
             nc.vector.tensor_tensor(
                 z_bf.rearrange("p (c i) j -> p c j i", i=2),
                 base_sb[:, :, cols].rearrange("p j (c i) -> p c j i", i=2),
@@ -345,11 +362,12 @@ def tile_list_landmark_gated_damping_kernel(
                 nc.sync.dma_start(out_rows[:, n0:n_end, starts[c] : starts[c] + w], result[:])
 
         for c in range(EARLY):
-            damp(PACK - 1, chunk(c), f"early_squares{c % 2}")
+            squares = placed([P, CHUNKS[c]], F32, f"early_squares{c % 2}", 2 * PASSES + (c % 2) / 2)
+            damp(PACK - 1, chunk(c), squares)
         quantize_states(0, states(0))
         for c in range(len(CHUNKS)):
             if EARLY <= c + LAG < len(CHUNKS):
-                damp(PACK - 1, chunk(c + LAG), rooms[c])
+                damp(PACK - 1, chunk(c + LAG), held([P, CHUNKS[c + LAG]], F32, rooms[c]))
             ahead = states(c + 1) if c + 1 < len(CHUNKS) else None
             project(c)
             if ahead is not None:

@@ -21,12 +21,16 @@ PACK = 4
 PASSES = K // (P * PACK)
 HALF = S // 2
 BANK = 512
+BANKS = 8
+REGION = T * 4
+
 CHUNKS = (128, 128, 256, 512, 512, 512)
+NARROW = 3
 EARLY = 4
 LAG = 3
 VECTOR_BANKS = (0, 0, 1, 1, 1, 3)
 STAGES = 12
-NARROW = 3
+
 GATE_BANKS = ((0, 3), (1, 0), (2, 1), (3, 0))
 VALUE_BANKS = ((2, 0), (3, 1), (4, 5), (6, 7))
 
@@ -48,20 +52,20 @@ def tile_list_landmark_gated_damping_kernel(
         picks = lists.tile([P, S // 16], U16, name="picks")
         places = lists.tile([P, S // 16], U16, name="places")
 
-        def placed(shape, dtype, name, slot):
-            return shared.tile(shape, dtype, name=name, align_bytes=64, offset=int(slot * T * 4))
+        def placed(shape, dtype, name, offset):
+            return shared.tile(shape, dtype, name=name, align_bytes=64, offset=offset)
 
-        tab_w = [placed([P, T], I32, f"tab_w{a}", a) for a in range(PASSES)]
-        wv_raw = [placed([P, PACK, H], F32, f"wv_raw{a}", PASSES + a) for a in range(PASSES)]
+        squares_at = 2 * PASSES * REGION
+        tab_w = [placed([P, T], I32, f"tab_w{a}", a * REGION) for a in range(PASSES)]
+        wv_raw = [placed([P, PACK, H], F32, f"wv_raw{a}", (PASSES + a) * REGION) for a in range(PASSES)]
         tab_rows = held([P, T // 4], I32, "tab_rows")
         key_s = held([P, PASSES, S // 4], I32, "key_s")
         wg_raw_w = held([P, PASSES, H // 2], I32, "wg_raw_w")
         wg_raw_s = held([P, PASSES, H // 4], I32, "wg_raw_s")
         weights = [held([P, S], F32, f"weights{t}") for t in range(PACK)]
-        wo_raw = placed([P, PACK, N], F32, "wo_raw", 2 * PASSES)
+        wo_raw = placed([P, PACK, N], F32, "wo_raw", squares_at)
         starts = [sum(CHUNKS[:c]) for c in range(len(CHUNKS))]
         base_sb = held([P, PACK, T2], F32, "base_sb")
-        warm = held([P, 2], F32, "warm")
         pages = [held([P, T2], F32, f"page{i}") for i in range(2)]
 
         nc.gpsimd.memset(wg_raw_s[:], 0)
@@ -69,8 +73,6 @@ def tile_list_landmark_gated_damping_kernel(
         nc.gpsimd.memset(tab_rows[64:128, :], 0)
         nc.gpsimd.memset(key_s[:], 0)
         nc.gpsimd.memset(pages[0][:], 0.0)
-        nc.vector.memset(warm[:, 0:1], 0.0)
-        nc.scalar.activation(warm[:, 1:2], warm[:, 0:1], ACT.Sigmoid)
         nc.vector.memset(pages[1][:, 0 : T2 // 2 + 1], 0.0)
         nc.vector.memset(pages[1][:, T2 // 2 + 1 : T2], 0.0)
 
@@ -81,11 +83,11 @@ def tile_list_landmark_gated_damping_kernel(
             rows = wv[a * P * PACK : (a + 1) * P * PACK, :]
             nc.sync.dma_start(wv_raw[a][:], rows.rearrange("(p j) c -> p j c", j=PACK))
 
-        def load_scales(tile, scales):
+        def load_wg_scales():
             for q in range(4):
                 nc.sync.dma_start(
-                    tile[32 * q : 32 * q + 4, :, :],
-                    scales.bitcast(I32)[:, 4 * q : 4 * q + 4, :].rearrange("a r w -> r a w"),
+                    wg_raw_s[32 * q : 32 * q + 4, :, :],
+                    wg_scales.bitcast(I32)[:, 4 * q : 4 * q + 4, :].rearrange("a r w -> r a w"),
                 )
 
         first_weights = held([P, HALF], F32, "first_weights")
@@ -102,11 +104,9 @@ def tile_list_landmark_gated_damping_kernel(
         key_w = [[held([P, HALF], U32, f"key_w{a}_{s}") for s in range(2)] for a in range(PASSES)]
         picked_rows = held([P, S], U8, "picked_rows")
 
-        def half_of(offsets, s):
-            return offsets[:, s * HALF // 16 : (s + 1) * HALF // 16]
-
         def gather_words(a, s):
-            nc.vector.tensor_copy(key_w[a][s][:], tab_w[a][:].bitcast(U32).indirect(half_of(picks, s)))
+            offsets = picks[:, s * HALF // 16 : (s + 1) * HALF // 16]
+            nc.vector.tensor_copy(key_w[a][s][:], tab_w[a][:].bitcast(U32).indirect(offsets))
 
         def gather_scales():
             nc.vector.tensor_copy(picked_rows[:], tab_rows[:].bitcast(U8).indirect(picks[:]))
@@ -122,7 +122,7 @@ def tile_list_landmark_gated_damping_kernel(
         nc.sync.dma_start(tab_rows[0:32, :], tab_scales.bitcast(I32).rearrange("a q w -> q a w"))
         load_words(0)
         nc.sync.dma_start(wg_raw_w[:], wg_words.bitcast(I32).rearrange("a p w -> p a w"))
-        load_scales(wg_raw_s, wg_scales)
+        load_wg_scales()
         load_words(1)
         gather_scales()
         load_wv(0)
@@ -173,7 +173,6 @@ def tile_list_landmark_gated_damping_kernel(
             )
 
         gated = [held([P, S], F32, f"gated{t}") for t in range(PACK)]
-
         values = [stage.tile([P, S], F32, name=f"values{t}", offset=t * S * 4) for t in range(PACK)]
 
         def gate(t, s):
@@ -193,9 +192,10 @@ def tile_list_landmark_gated_damping_kernel(
             nc.scalar.activation(gated[t][:, s * HALF : (s + 1) * HALF], acc[:], ACT.Sigmoid)
 
         def value(t, s):
+            first = (t, s) == (0, 0)
             cols = slice(t * P, (t + 1) * P)
             acc = psum.tile([P, BANK], F32, name=f"bank{VALUE_BANKS[t][s]}")
-            order = (0, 1) if (t, s) == (0, 0) else (1, 0)
+            order = (0, 1) if first else (1, 0)
             for a in order:
                 nc.tensor.matmul_mx(
                     out=acc[:],
@@ -206,9 +206,8 @@ def tile_list_landmark_gated_damping_kernel(
                     start=(a == order[0]),
                     stop=(a == order[-1]),
                 )
-            half = gated[t][:, s * HALF : (s + 1) * HALF]
-            if (t, s) == (0, 0):
-                nc.vector.tensor_tensor(half, acc[:], half, MULT)
+            if first:
+                nc.vector.tensor_tensor(gated[0][:, 0:HALF], acc[:], gated[0][:, 0:HALF], MULT)
             else:
                 nc.scalar.copy(values[t][:, s * HALF : (s + 1) * HALF], acc[:])
 
@@ -232,6 +231,9 @@ def tile_list_landmark_gated_damping_kernel(
             nc.scalar.activation(squares[:], pages[t % 2][:, cols], ACT.Square)
             nc.scalar.activation(factors[:, t, cols], squares[:], ACT.Abs_reciprocal_sqrt, bias=1.0)
 
+        def damp_plane(t):
+            damp(t, slice(0, T2), placed([P, T2], F32, "squares", squares_at))
+
         gather_words(0, 0)
         gather_words(0, 1)
         permute_wg_scales()
@@ -246,11 +248,12 @@ def tile_list_landmark_gated_damping_kernel(
         nc.vector.tensor_tensor(gated[0][:, 0:HALF], gated[0][:, 0:HALF], first_weights[:], MULT)
         value(0, 0)
         scatter(0, 0, 1)
-        for t, s in ((1, 0), (0, 1), (1, 1)):
+        next_halves = ((1, 0), (0, 1), (1, 1))
+        for t, s in next_halves:
             value(t, s)
         gate(0, 1)
         gate(1, 1)
-        for t, s in ((1, 0), (0, 1), (1, 1)):
+        for t, s in next_halves:
             combine(t, s, s + 1)
             scatter(t, s, s + 1)
         for t in range(2, PACK):
@@ -264,10 +267,10 @@ def tile_list_landmark_gated_damping_kernel(
             ACT.Copy,
         )
         for t in range(2, PACK):
-            damp(t - 2, slice(0, T2), placed([P, T2], F32, "squares", 2 * PASSES))
+            damp_plane(t - 2)
             combine(t, 0, 2)
             scatter(t, 0, 2)
-        damp(2, slice(0, T2), placed([P, T2], F32, "squares", 2 * PASSES))
+        damp_plane(2)
 
         wide = slice(starts[NARROW], T2)
         pairs = held([P, 2, T2 - starts[NARROW], 2], BF16, "pairs")
@@ -276,7 +279,7 @@ def tile_list_landmark_gated_damping_kernel(
 
         wo_w = held([P, N], U32, f"gated{PACK - 1}")
         wo_s = held([P, N], U8, "wo_s")
-        for n0, n1 in ((0, 512), (512, N)):
+        for n0, n1 in ((0, BANK), (BANK, N)):
             nc.vector.quantize_mx(
                 out=wo_w[:, n0:n1].bitcast(FP8X4),
                 scales=wo_s[:, n0:n1],
@@ -284,91 +287,91 @@ def tile_list_landmark_gated_damping_kernel(
             )
 
         out_rows = out.rearrange("(n p) t -> p n t", p=P)
-
         z_words = held([P, T2], U32, "z_words")
         z_scales = held([P, T2], U8, "tab_rows")
-        rooms = ["room0", "room0", "room2", "weights0", "weights1", "weights2"]
+        z_names = ["z_first", "z_first", "z_third", "weights0", "weights1", "weights2"]
 
         def chunk(c):
             return slice(starts[c], starts[c] + CHUNKS[c])
 
-        def states(c):
+        def halves(cols):
+            middle = (cols.start + cols.stop) // 2
+            return (slice(cols.start, middle), slice(middle, cols.stop))
+
+        def shifted(cols, first):
+            return slice(cols.start - first, cols.stop - first)
+
+        def form_z(c):
             cols = chunk(c)
-            z_tile = held([P, CHUNKS[c], PACK], BF16, rooms[c])
-            z_bf = z_tile[:]
-            if c >= NARROW:
-                own = slice(cols.start - wide.start, cols.stop - wide.start)
+            z_bf = held([P, CHUNKS[c], PACK], BF16, z_names[c])
+            if c < NARROW:
                 nc.vector.tensor_tensor(
-                    pairs[:, 1, own, :].rearrange("p (c i) j -> p c j i", i=4),
-                    base_sb[:, 2:PACK, cols].rearrange("p j (c i) -> p c j i", i=4),
-                    factors[:, 2:PACK, cols].rearrange("p j (c i) -> p c j i", i=4),
+                    z_bf[:].rearrange("p (c i) j -> p c j i", i=2),
+                    base_sb[:, :, cols].rearrange("p j (c i) -> p c j i", i=2),
+                    factors[:, :, cols].rearrange("p j (c i) -> p c j i", i=2),
                     MULT,
                 )
-                nc.vector.tensor_copy(
-                    z_bf.bitcast(I32).rearrange("p (c i) h -> p c h i", i=2),
-                    pairs[:].rearrange("p h c j -> p h (c j)").bitcast(I32)[:, :, own].rearrange("p h (c i) -> p c h i", i=2),
-                )
                 return z_bf
-            nc.vector.tensor_tensor(
-                z_bf.rearrange("p (c i) j -> p c j i", i=2),
-                base_sb[:, :, cols].rearrange("p j (c i) -> p c j i", i=2),
-                factors[:, :, cols].rearrange("p j (c i) -> p c j i", i=2),
-                MULT,
-            )
+            for part in halves(cols):
+                nc.vector.tensor_tensor(
+                    pairs[:, 1, shifted(part, wide.start), :].rearrange("p (c i) j -> p c j i", i=4),
+                    base_sb[:, 2:PACK, part].rearrange("p j (c i) -> p c j i", i=4),
+                    factors[:, 2:PACK, part].rearrange("p j (c i) -> p c j i", i=4),
+                    MULT,
+                )
+            pair_words = pairs[:].rearrange("p h c j -> p h (c j)").bitcast(I32)
+            for part in halves(cols):
+                nc.vector.tensor_copy(
+                    z_bf[:, shifted(part, cols.start), :].bitcast(I32).rearrange("p (c i) h -> p c h i", i=2),
+                    pair_words[:, :, shifted(part, wide.start)].rearrange("p h (c i) -> p c h i", i=2),
+                )
             return z_bf
 
-        def quantize_states(c, z_bf):
-            nc.vector.quantize_mx(
-                out=z_words[:, chunk(c)].bitcast(FP8X4),
-                scales=z_scales[:, chunk(c)],
-                in_=z_bf.rearrange("p c j -> p (c j)"),
-            )
+        def quantize_z(c, z_bf):
+            for part in (chunk(c),) if c < NARROW else halves(chunk(c)):
+                nc.vector.quantize_mx(
+                    out=z_words[:, part].bitcast(FP8X4),
+                    scales=z_scales[:, part],
+                    in_=z_bf[:, shifted(part, starts[c]), :].rearrange("p c j -> p (c j)"),
+                )
 
-        used = []
+        filled = []
 
         def project(c):
-            z_w = z_words[:, chunk(c)]
-            z_s = z_scales[:, chunk(c)]
-            w = CHUNKS[c]
-            per_bank = 2 if w < BANK else 1
-            per_store = per_bank
-            firsts = list(range(0, N // P, per_bank))
-            for n0 in range(0, N // P, per_store):
-                n_end = min(n0 + per_store, N // P)
-                slot = len(used) % STAGES
-                result = stage.tile([P, n_end - n0, w], F32, name=f"result{slot}", offset=slot * BANK * 4)
-                for n1 in range(n0, n_end, per_bank):
-                    count = min(per_bank, n_end - n1)
-                    acc = psum.tile([P, count, w], F32, name=f"bank{len(used) % 8}")
-                    used.append(n1)
-                    for i in range(count):
-                        rows = slice((n1 + i) * P, (n1 + i + 1) * P)
-                        nc.tensor.matmul_mx(
-                            out=acc[:, i, :],
-                            lhsT=wo_w[:, rows].bitcast(FP8X4),
-                            lhsT_scale=wo_s[:, rows],
-                            rhs=z_w.bitcast(FP8X4),
-                            rhs_scale=z_s,
-                            start=True,
-                            stop=True,
-                        )
-                    part = result[:, n1 - n0 : n1 - n0 + count, :]
-                    bank = firsts.index(n1)
-                    share = VECTOR_BANKS[c]
-                    if bank * share % len(firsts) < share:
-                        nc.vector.tensor_copy(part, acc[:])
-                    else:
-                        nc.scalar.copy(part, acc[:])
-                nc.sync.dma_start(out_rows[:, n0:n_end, starts[c] : starts[c] + w], result[:])
+            width = CHUNKS[c]
+            per_bank = 2 if c < NARROW else 1
+            banks = N // P // per_bank
+            share = VECTOR_BANKS[c]
+            for bank in range(banks):
+                n0 = bank * per_bank
+                slot = len(filled) % STAGES
+                result = stage.tile([P, per_bank, width], F32, name=f"result{slot}", offset=slot * BANK * 4)
+                acc = psum.tile([P, per_bank, width], F32, name=f"bank{len(filled) % BANKS}")
+                filled.append(n0)
+                for i in range(per_bank):
+                    rows = slice((n0 + i) * P, (n0 + i + 1) * P)
+                    nc.tensor.matmul_mx(
+                        out=acc[:, i, :],
+                        lhsT=wo_w[:, rows].bitcast(FP8X4),
+                        lhsT_scale=wo_s[:, rows],
+                        rhs=z_words[:, chunk(c)].bitcast(FP8X4),
+                        rhs_scale=z_scales[:, chunk(c)],
+                        start=True,
+                        stop=True,
+                    )
+                if (bank - 1) * share % banks < share:
+                    nc.vector.tensor_copy(result[:], acc[:])
+                else:
+                    nc.scalar.copy(result[:], acc[:])
+                nc.sync.dma_start(out_rows[:, n0 : n0 + per_bank, chunk(c)], result[:])
 
         for c in range(EARLY):
-            squares = placed([P, CHUNKS[c]], F32, f"early_squares{c % 2}", 2 * PASSES + (c % 2) / 2)
+            squares = placed([P, CHUNKS[c]], F32, f"early_squares{c % 2}", squares_at + c % 2 * REGION // 2)
             damp(PACK - 1, chunk(c), squares)
-        quantize_states(0, states(0))
+        quantize_z(0, form_z(0))
         for c in range(len(CHUNKS)):
             if EARLY <= c + LAG < len(CHUNKS):
-                damp(PACK - 1, chunk(c + LAG), held([P, CHUNKS[c + LAG]], F32, rooms[c]))
-            ahead = states(c + 1) if c + 1 < len(CHUNKS) else None
+                damp(PACK - 1, chunk(c + LAG), held([P, CHUNKS[c + LAG]], F32, z_names[c]))
+            if c + 1 < len(CHUNKS):
+                quantize_z(c + 1, form_z(c + 1))
             project(c)
-            if ahead is not None:
-                quantize_states(c + 1, ahead)

@@ -22,17 +22,31 @@ PASSES = K // (P * PACK)
 HALF = S // 2
 BANK = 512
 BANKS = 8
-REGION = T * 4
+KB = 1024
+
+ZEROED = 1536
+FIRST = 256
+REST = T2 - FIRST
+STEP = 256
+WO_SPLIT = 512
 
 CHUNKS = (128, 128, 256, 512, 512, 512)
-NARROW = 3
-EARLY = 4
-LAG = 3
-VECTOR_BANKS = (0, 0, 1, 1, 1, 3)
-STAGES = 12
+VECTOR_BANKS = ((), (), (), (1,), (1, 4), (1, 3, 5))
 
-GATE_BANKS = ((0, 3), (1, 0), (2, 1), (3, 0))
-VALUE_BANKS = ((2, 0), (3, 1), (4, 5), (6, 7))
+AT_TAB = 0
+AT_WV = 16 * KB
+AT_BASE = 32 * KB
+AT_PAGES = 64 * KB
+AT_WEIGHTS = 80 * KB
+AT_GATED = 96 * KB
+AT_VALUES = 102 * KB
+AT_SPARE = 116 * KB
+AT_LAST = 128 * KB
+AT_WO_A = 134 * KB
+AT_SQUARES = 140 * KB
+AT_WO_B = 149 * KB
+AT_ROUNDED = 157 * KB
+AT_KEYS = 165 * KB
 
 
 def tile_list_landmark_gated_damping_kernel(
@@ -43,38 +57,40 @@ def tile_list_landmark_gated_damping_kernel(
         lists = ctx.enter_context(tc.tile_pool(name="lists", bufs=1))
         shared = ctx.enter_context(tc.tile_pool(name="shared", bufs=1))
         keep = ctx.enter_context(tc.tile_pool(name="keep", bufs=1))
-        stage = ctx.enter_context(tc.tile_pool(name="stage", bufs=1))
         psum = ctx.enter_context(tc.psum_pool(name="psum", bufs=1))
 
         def held(shape, dtype, name):
             return keep.tile(shape, dtype, name=name, align_bytes=64)
 
-        picks = lists.tile([P, S // 16], U16, name="picks")
-        places = lists.tile([P, S // 16], U16, name="places")
-
         def placed(shape, dtype, name, offset):
             return shared.tile(shape, dtype, name=name, align_bytes=64, offset=offset)
 
-        squares_at = 2 * PASSES * REGION
-        tab_w = [placed([P, T], I32, f"tab_w{a}", a * REGION) for a in range(PASSES)]
-        wv_raw = [placed([P, PACK, H], F32, f"wv_raw{a}", (PASSES + a) * REGION) for a in range(PASSES)]
+        def bank(i, shape):
+            return psum.tile(shape, F32, name=f"bank{i}")
+
+        picks = lists.tile([P, S // 16], U16, name="picks")
+        places = lists.tile([P, S // 16], U16, name="places")
+
+        tab_w = [placed([P, T], I32, f"tab_w{a}", AT_TAB + a * 8 * KB) for a in range(PASSES)]
+        wv_raw = [placed([P, PACK, H], F32, f"wv_raw{a}", AT_WV + a * 8 * KB) for a in range(PASSES)]
+        base_sb = placed([P, PACK, T2], F32, "base_sb", AT_BASE)
+        pages = [placed([P, T2], F32, f"page{i}", AT_PAGES + i * 8 * KB) for i in range(2)]
         tab_rows = held([P, T // 4], I32, "tab_rows")
         key_s = held([P, PASSES, S // 4], I32, "key_s")
         wg_raw_w = held([P, PASSES, H // 2], I32, "wg_raw_w")
         wg_raw_s = held([P, PASSES, H // 4], I32, "wg_raw_s")
-        weights = [held([P, S], F32, f"weights{t}") for t in range(PACK)]
-        wo_raw = placed([P, PACK, N], F32, "wo_raw", squares_at)
-        starts = [sum(CHUNKS[:c]) for c in range(len(CHUNKS))]
-        base_sb = held([P, PACK, T2], F32, "base_sb")
-        pages = [held([P, T2], F32, f"page{i}") for i in range(2)]
 
         nc.gpsimd.memset(wg_raw_s[:], 0)
         nc.gpsimd.memset(tab_rows[32:64, :], 0)
         nc.gpsimd.memset(tab_rows[64:128, :], 0)
         nc.gpsimd.memset(key_s[:], 0)
         nc.gpsimd.memset(pages[0][:], 0.0)
-        nc.vector.memset(pages[1][:, 0 : T2 // 2 + 1], 0.0)
-        nc.vector.memset(pages[1][:, T2 // 2 + 1 : T2], 0.0)
+        nc.gpsimd.memset(pages[1][:, ZEROED:T2], 0.0)
+        nc.vector.memset(pages[1][:, 0 : ZEROED // 2 + 1], 0.0)
+        nc.vector.memset(pages[1][:, ZEROED // 2 + 1 : ZEROED], 0.0)
+
+        pieces = [(0, 0, HALF), (0, HALF, S), (1, 0, HALF), (1, HALF, S), (2, 0, S), (3, 0, S)]
+        weights = {}
 
         def load_words(a):
             nc.sync.dma_start(tab_w[a][:], tab_words[a].rearrange("p t i -> p (t i)").bitcast(I32))
@@ -83,295 +99,343 @@ def tile_list_landmark_gated_damping_kernel(
             rows = wv[a * P * PACK : (a + 1) * P * PACK, :]
             nc.sync.dma_start(wv_raw[a][:], rows.rearrange("(p j) c -> p j c", j=PACK))
 
-        def load_wg_scales():
-            for q in range(4):
-                nc.sync.dma_start(
-                    wg_raw_s[32 * q : 32 * q + 4, :, :],
-                    wg_scales.bitcast(I32)[:, 4 * q : 4 * q + 4, :].rearrange("a r w -> r a w"),
-                )
-
-        first_weights = held([P, HALF], F32, "first_weights")
-
-        def load_weights(t, cols):
-            tile = first_weights if (t, cols.stop) == (0, HALF) else weights[t]
-            rows = wgs.rearrange("(u t e) j -> t u e j", t=PACK, e=2)[t, :, :, cols]
+        def load_weights(t, j0, j1):
+            tile = placed([P, j1 - j0], F32, f"weights{t}_{j0}", AT_WEIGHTS + (t * S + j0) * 4)
+            rows = wgs.rearrange("(u t e) j -> t u e j", t=PACK, e=2)[t, :, :, j0:j1]
             for q in (0, 2, 1, 3):
-                nc.sync.dma_start(tile[32 * q : 32 * q + 32, cols], rows)
+                nc.sync.dma_start(tile[32 * q : 32 * q + 32, :], rows)
+            for j in range(j0, j1, HALF):
+                weights[t, j] = (tile, j - j0)
+
+        def weights_of(t, j0, j1):
+            tile, first = weights[t, j0]
+            return tile[:, first : first + j1 - j0]
 
         def load_plane(tile, source, t):
             nc.sync.dma_start(tile[:, t, :], source.rearrange("(u t e) c -> t u e c", t=PACK, e=2)[t])
 
-        key_w = [[held([P, HALF], U32, f"key_w{a}_{s}") for s in range(2)] for a in range(PASSES)]
+        key_w = [
+            [placed([P, HALF], U32, f"key_w{a}_{s}", AT_KEYS + (2 * a + s) * 2 * KB) for s in range(2)]
+            for a in range(PASSES)
+        ]
         picked_rows = held([P, S], U8, "picked_rows")
 
         def gather_words(a, s):
             offsets = picks[:, s * HALF // 16 : (s + 1) * HALF // 16]
             nc.vector.tensor_copy(key_w[a][s][:], tab_w[a][:].bitcast(U32).indirect(offsets))
 
-        def gather_scales():
-            nc.vector.tensor_copy(picked_rows[:], tab_rows[:].bitcast(U8).indirect(picks[:]))
-            for q in (0, 2, 1, 3):
-                nc.sync.dma_start(
-                    key_s[32 * q : 32 * q + 4, :, :], picked_rows[:].bitcast(I32)[8 * q : 8 * q + 8, :]
-                )
-
         def key_scales(a, s):
             return key_s[:, a, s * HALF // 4 : (s + 1) * HALF // 4].bitcast(U8)
+
+        wo_cols = ((0, WO_SPLIT), (WO_SPLIT, N))
+        wo_raw = [
+            placed([P, PACK, n1 - n0], F32, f"wo_raw{n0}", at) for (n0, n1), at in zip(wo_cols, (AT_WO_A, AT_WO_B))
+        ]
+
+        def load_wo(part):
+            n0, n1 = wo_cols[part]
+            for t in range(PACK):
+                load_plane(wo_raw[part], wo[:, n0:n1], t)
 
         nc.sync.dma_start(picks[:], offs)
         nc.sync.dma_start(tab_rows[0:32, :], tab_scales.bitcast(I32).rearrange("a q w -> q a w"))
         load_words(0)
         nc.sync.dma_start(wg_raw_w[:], wg_words.bitcast(I32).rearrange("a p w -> p a w"))
-        load_wg_scales()
+        for q in range(4):
+            nc.sync.dma_start(
+                wg_raw_s[32 * q : 32 * q + 4, :, :],
+                wg_scales.bitcast(I32)[:, 4 * q : 4 * q + 4, :].rearrange("a r w -> r a w"),
+            )
         load_words(1)
-        gather_scales()
+        nc.vector.tensor_copy(picked_rows[:], tab_rows[:].bitcast(U8).indirect(picks[:]))
+        for q in (0, 2, 1, 3):
+            nc.sync.dma_start(key_s[32 * q : 32 * q + 4, :, :], picked_rows[:].bitcast(I32)[8 * q : 8 * q + 8, :])
         load_wv(0)
         load_wv(1)
+        load_weights(0, 0, HALF)
         nc.sync.dma_start(places[:], offs2)
-        load_weights(0, slice(0, HALF))
-        load_weights(1, slice(0, HALF))
-        load_weights(0, slice(HALF, S))
-        load_weights(1, slice(HALF, S))
-        for t in range(PACK):
-            load_plane(wo_raw, wo, t)
-        load_weights(2, slice(0, S))
-        load_weights(3, slice(0, S))
-        for t in range(PACK):
+        load_weights(0, HALF, S)
+        load_weights(1, 0, S)
+        load_wo(0)
+        load_weights(2, 0, S)
+        load_weights(3, 0, S)
+        for t in range(PACK - 1):
             load_plane(base_sb, base, t)
+        load_wo(1)
+        load_plane(base_sb, base, PACK - 1)
 
-        wg_w = held([P, PASSES, H // 2], I32, "wg_w")
+        wg_w = [held([P, PASSES, H // 4], I32, "wg_w")]
         wg_s = held([P, PASSES, H], U8, "wg_s")
+        nc.gpsimd.tensor_copy(
+            wg_s[:].rearrange("p a (t u e) -> p a t u e", t=PACK, e=2),
+            wg_raw_s[:].bitcast(U8).rearrange("p a (u t e) -> p a t u e", t=PACK, e=2),
+        )
 
-        def permute_wg_words():
-            nc.gpsimd.tensor_copy(
-                wg_w[:].rearrange("p a (t u) -> p a t u", t=PACK),
-                wg_raw_w[:].rearrange("p a (u t) -> p a t u", t=PACK),
+        def permute_wg_words(half, copy):
+            copy(
+                wg_w[half][:].rearrange("p a (t u) -> p a t u", t=2),
+                wg_raw_w[:].rearrange("p a (u t) -> p a t u", t=PACK)[:, :, 2 * half : 2 * half + 2, :],
             )
 
-        def permute_wg_scales():
-            nc.gpsimd.tensor_copy(
-                wg_s[:].rearrange("p a (t u e) -> p a t u e", t=PACK, e=2),
-                wg_raw_s[:].bitcast(U8).rearrange("p a (u t e) -> p a t u e", t=PACK, e=2),
-            )
+        permute_wg_words(0, nc.gpsimd.tensor_copy)
 
-        wv_w = [held([P, H], U32, f"wv_w{a}") for a in range(PASSES)]
-        wv_s = [held([P, H], U8, f"wv_s{a}") for a in range(PASSES)]
+        wv_codes = {}
 
         def round_wv(a, t0, t1, copy):
-            rounded = held([P, t1 - t0, P, PACK], BF16, f"wv_bf{a}_{t0}")
+            rounded = placed([P, t1 - t0, P, PACK], BF16, f"wv_bf{a}_{t0}", AT_ROUNDED + (PACK * a + t0) * KB)
             copy(
                 rounded[:].rearrange("p t (u e) j -> p u t j e", e=2),
                 wv_raw[a][:].rearrange("p j (u t e) -> p u t j e", t=PACK, e=2)[:, :, t0:t1, :, :],
             )
             return rounded
 
-        def quantize_wv(a, t0, t1, rounded):
+        def quantize_wv(a, t0, t1, rounded, words):
+            scales = held([P, (t1 - t0) * P], U8, f"wv_s{a}_{t0}")
             nc.vector.quantize_mx(
-                out=wv_w[a][:, t0 * P : t1 * P].bitcast(FP8X4),
-                scales=wv_s[a][:, t0 * P : t1 * P],
-                in_=rounded[:].rearrange("p t m j -> p (t m j)"),
+                out=words[:].bitcast(FP8X4), scales=scales[:], in_=rounded[:].rearrange("p t m j -> p (t m j)")
             )
+            for t in range(t0, t1):
+                cols = slice((t - t0) * P, (t - t0 + 1) * P)
+                wv_codes[a, t] = (words[:, cols].bitcast(FP8X4), scales[:, cols])
 
-        gated = [held([P, S], F32, f"gated{t}") for t in range(PACK)]
-        values = [stage.tile([P, S], F32, name=f"values{t}", offset=t * S * 4) for t in range(PACK)]
+        def wv_words(a, t0, t1):
+            return held([P, (t1 - t0) * P], U32, f"wv_w{a}_{t0}")
 
-        def gate(t, s):
-            cols = slice(t * P, (t + 1) * P)
-            acc = psum.tile([P, BANK], F32, name=f"bank{GATE_BANKS[t][s]}")
+        def gate(t, s, at_bank, target):
+            acc = bank(at_bank, [P, BANK])
             order = (1, 0)
             for a in order:
                 nc.tensor.matmul_mx(
                     out=acc[:],
-                    lhsT=wg_w[:, a, t * P // 2 : (t + 1) * P // 2].bitcast(FP4X4),
-                    lhsT_scale=wg_s[:, a, cols],
+                    lhsT=wg_w[t // 2][:, a, t % 2 * P // 2 : (t % 2 + 1) * P // 2].bitcast(FP4X4),
+                    lhsT_scale=wg_s[:, a, t * P : (t + 1) * P],
                     rhs=key_w[a][s][:].bitcast(FP8X4),
                     rhs_scale=key_scales(a, s),
                     start=(a == order[0]),
                     stop=(a == order[-1]),
                 )
-            nc.scalar.activation(gated[t][:, s * HALF : (s + 1) * HALF], acc[:], ACT.Sigmoid)
+            nc.scalar.activation(target, acc[:], ACT.Sigmoid)
 
-        def value(t, s):
-            first = (t, s) == (0, 0)
-            cols = slice(t * P, (t + 1) * P)
-            acc = psum.tile([P, BANK], F32, name=f"bank{VALUE_BANKS[t][s]}")
-            order = (0, 1) if first else (1, 0)
-            for a in order:
-                nc.tensor.matmul_mx(
-                    out=acc[:],
-                    lhsT=wv_w[a][:, cols].bitcast(FP8X4),
-                    lhsT_scale=wv_s[a][:, cols],
-                    rhs=key_w[a][s][:].bitcast(FP8X4),
-                    rhs_scale=key_scales(a, s),
-                    start=(a == order[0]),
-                    stop=(a == order[-1]),
-                )
-            if first:
-                nc.vector.tensor_tensor(gated[0][:, 0:HALF], acc[:], gated[0][:, 0:HALF], MULT)
-            else:
-                nc.scalar.copy(values[t][:, s * HALF : (s + 1) * HALF], acc[:])
+        def value_pass(acc, t, s, a, start):
+            codes, scales = wv_codes[a, t]
+            nc.tensor.matmul_mx(
+                out=acc[:],
+                lhsT=codes,
+                lhsT_scale=scales,
+                rhs=key_w[a][s][:].bitcast(FP8X4),
+                rhs_scale=key_scales(a, s),
+                start=start,
+                stop=not start,
+            )
 
-        def combine(t, s0, s1):
-            for s in range(s0, s1):
-                cols = slice(s * HALF, (s + 1) * HALF)
-                weighed = gated[t][:, cols]
-                if (t, s) == (1, 0):
-                    weighed = held([P, HALF], F32, "first_weights")[:]
-                nc.gpsimd.tensor_tensor(weighed, gated[t][:, cols], weights[t][:, cols], MULT)
-                nc.gpsimd.tensor_tensor(gated[t][:, cols], weighed, values[t][:, cols], MULT)
+        def value(t, s, at_bank, target):
+            acc = bank(at_bank, [P, BANK])
+            value_pass(acc, t, s, 1, True)
+            value_pass(acc, t, s, 0, False)
+            nc.scalar.copy(target, acc[:])
 
-        def scatter(t, s0, s1):
-            cols = slice(s0 * HALF, s1 * HALF)
-            offsets = places[:, s0 * HALF // 16 : s1 * HALF // 16]
-            nc.vector.tensor_copy(pages[t % 2][:].indirect(offsets), gated[t][:, cols])
-
-        factors = placed([P, PACK, T2], F32, "factors", 0)
-
-        def damp(t, cols, squares):
-            nc.scalar.activation(squares[:], pages[t % 2][:, cols], ACT.Square)
-            nc.scalar.activation(factors[:, t, cols], squares[:], ACT.Abs_reciprocal_sqrt, bias=1.0)
-
-        def damp_plane(t):
-            damp(t, slice(0, T2), placed([P, T2], F32, "squares", squares_at))
+        def scatter(piece, source):
+            t, j0, j1 = pieces[piece]
+            nc.vector.tensor_copy(pages[t % 2][:].indirect(places[:, j0 // 16 : j1 // 16]), source)
 
         gather_words(0, 0)
         gather_words(0, 1)
-        permute_wg_scales()
-        permute_wg_words()
         gather_words(1, 0)
         gather_words(1, 1)
-        gate(0, 0)
-        gate(1, 0)
-        quantize_wv(0, 0, PACK, round_wv(0, 0, PACK, nc.vector.tensor_copy))
-        quantize_wv(1, 0, 2, round_wv(1, 0, 2, nc.vector.tensor_copy))
-        quantize_wv(1, 2, PACK, round_wv(1, 2, PACK, nc.scalar.copy))
-        nc.vector.tensor_tensor(gated[0][:, 0:HALF], gated[0][:, 0:HALF], first_weights[:], MULT)
-        value(0, 0)
-        scatter(0, 0, 1)
-        next_halves = ((1, 0), (0, 1), (1, 1))
-        for t, s in next_halves:
-            value(t, s)
-        gate(0, 1)
-        gate(1, 1)
-        for t, s in next_halves:
-            combine(t, s, s + 1)
-            scatter(t, s, s + 1)
-        for t in range(2, PACK):
-            for s in range(2):
-                gate(t, s)
-                value(t, s)
-        wo_bf = held([P, N, PACK], BF16, "wo_bf")
-        nc.scalar.activation(
-            wo_bf[:].rearrange("p (c i) j -> p c j i", i=2),
-            wo_raw[:].rearrange("p j (c i) -> p c j i", i=2),
-            ACT.Copy,
-        )
-        for t in range(2, PACK):
-            damp_plane(t - 2)
-            combine(t, 0, 2)
-            scatter(t, 0, 2)
-        damp_plane(2)
+        rounded = [round_wv(0, t, t + 2, nc.vector.tensor_copy) for t in (0, 2)]
+        quantize_wv(0, 0, 2, rounded[0], wv_words(0, 0, 2))
+        quantize_wv(0, 2, PACK, rounded[1], wv_words(0, 2, PACK))
 
-        wide = slice(starts[NARROW], T2)
-        pairs = held([P, 2, T2 - starts[NARROW], 2], BF16, "pairs")
+        gated = [placed([P, HALF], F32, f"gated{i}", AT_SPARE + i * 2 * KB) for i in range(4)]
+        gated.append(placed([P, S], F32, "gated4", AT_GATED + 2 * KB))
+        gated.append(placed([P, S], F32, "gated5", AT_LAST))
+        values = [None] + [placed([P, HALF], F32, f"values{i}", AT_VALUES + (i - 1) * 2 * KB) for i in range(1, 4)]
+        gate(0, 0, 0, gated[0][:])
+        gate(1, 0, 1, gated[2][:])
+        gate(0, 1, 2, gated[1][:])
+        early = [bank(3 + s, [P, BANK]) for s in range(2)]
+        for s in range(2):
+            value_pass(early[s], 0, s, 0, True)
+        rounded = [round_wv(1, t, t + 1, nc.vector.tensor_copy) for t in range(2)]
+        rounded.append(round_wv(1, 2, PACK, nc.scalar.copy))
         for t in range(2):
-            nc.gpsimd.tensor_tensor(pairs[:, 0, :, t], base_sb[:, t, wide], factors[:, t, wide], MULT)
-
-        wo_w = held([P, N], U32, f"gated{PACK - 1}")
-        wo_s = held([P, N], U8, "wo_s")
-        for n0, n1 in ((0, BANK), (BANK, N)):
-            nc.vector.quantize_mx(
-                out=wo_w[:, n0:n1].bitcast(FP8X4),
-                scales=wo_s[:, n0:n1],
-                in_=wo_bf[:, n0:n1, :].rearrange("p n j -> p (n j)"),
+            quantize_wv(1, t, t + 1, rounded[t], wv_words(1, t, t + 1))
+        for s in range(2):
+            value_pass(early[s], 0, s, 1, False)
+        wg_w.append(placed([P, PASSES, H // 4], I32, "wg_late", AT_ROUNDED + PACK * KB))
+        permute_wg_words(1, nc.vector.tensor_copy)
+        nc.vector.tensor_tensor(gated[0][:], gated[0][:], weights_of(0, 0, HALF), MULT)
+        first_h = placed([P, HALF], F32, "first_h", AT_GATED)
+        nc.vector.tensor_tensor(first_h[:], early[0][:], gated[0][:], MULT)
+        scatter(0, first_h[:])
+        nc.scalar.copy(values[1][:], early[1][:])
+        quantize_wv(1, 2, PACK, rounded[2], placed([P, 2 * P], U32, "wv_late", AT_SPARE))
+        value(1, 0, 5, values[2][:])
+        value(1, 1, 6, values[3][:])
+        gate(1, 1, 3, gated[3][:])
+        for t, gate_banks in ((2, (7, 0)), (3, (1, 2))):
+            for s in range(2):
+                gate(t, s, gate_banks[s], gated[t + 2][:, s * HALF : (s + 1) * HALF])
+        def round_wo(part, rounded_wo):
+            nc.scalar.activation(
+                rounded_wo[:].rearrange("p (c i) j -> p c j i", i=2),
+                wo_raw[part][:].rearrange("p j (c i) -> p c j i", i=2),
+                ACT.Copy,
             )
 
-        out_rows = out.rearrange("(n p) t -> p n t", p=P)
+        wo_bf = [held([P, WO_SPLIT, PACK], BF16, "wo_bf0")]
+        round_wo(0, wo_bf[0])
+        values.extend(placed([P, S], F32, f"values{i}", AT_WO_A + (4 * i - 18) * KB) for i in (4, 5))
+        for t, value_banks in ((2, (4, 5)), (3, (6, 7))):
+            for s in range(2):
+                value(t, s, value_banks[s], values[t + 2][:, s * HALF : (s + 1) * HALF])
+
+        def combine(piece):
+            t, j0, j1 = pieces[piece]
+            weighed = gated[piece]
+            if piece == 1:
+                weighed = placed([P, HALF], F32, "weighed", AT_WEIGHTS)
+            nc.gpsimd.tensor_tensor(weighed[:], gated[piece][:], weights_of(t, j0, j1), MULT)
+            nc.gpsimd.tensor_tensor(gated[piece][:], weighed[:], values[piece][:], MULT)
+
+        first_factors = held([P, PACK, FIRST], F32, "first_factors")
+        early_factors = [placed([P, REST], F32, f"factors{t}", AT_TAB + t * 8 * KB) for t in range(2)]
+        late_factors = placed([P, 2, REST], F32, "late_factors", AT_WV)
+
+        def factors(t, c0, c1):
+            if c1 <= FIRST:
+                return first_factors[:, t, c0:c1]
+            if t < 2:
+                return early_factors[t][:, c0 - FIRST : c1 - FIRST]
+            return late_factors[:, t - 2, c0 - FIRST : c1 - FIRST]
+
+        def inverse_root(t, c0, c1, squares):
+            nc.scalar.activation(factors(t, c0, c1), squares, ACT.Abs_reciprocal_sqrt, bias=1.0)
+
+        def damp_plane(t, at):
+            squares = placed([P, T2], F32, f"squares{t}", at)
+            nc.scalar.activation(squares[:], pages[t % 2][:], ACT.Square)
+            inverse_root(t, 0, FIRST, squares[:, 0:FIRST])
+            inverse_root(t, FIRST, T2, squares[:, FIRST:T2])
+
+        for piece in range(1, 4):
+            combine(piece)
+            scatter(piece, gated[piece][:])
+            if piece % 2 == 1:
+                damp_plane(piece // 2, AT_SQUARES)
+        wo_bf.append(placed([P, N - WO_SPLIT, PACK], BF16, "wo_bf1", AT_SQUARES))
+        round_wo(1, wo_bf[1])
+        combine(4)
+        scatter(4, gated[4][:])
+        damp_plane(2, AT_WO_B)
+        combine(5)
+        scatter(5, gated[5][:])
+
+        pairs = held([P, 2, REST, 2], BF16, "pairs")
+        for t in range(2):
+            nc.gpsimd.tensor_tensor(pairs[:, 0, :, t], base_sb[:, t, FIRST:T2], early_factors[t][:], MULT)
+
+        wo_codes = []
+
+        def quantize_wo(part, at):
+            n0, n1 = wo_cols[part]
+            words = placed([P, n1 - n0], U32, f"wo_w{part}", at)
+            scales = held([P, n1 - n0], U8, f"wo_s{part}")
+            nc.vector.quantize_mx(
+                out=words[:].bitcast(FP8X4), scales=scales[:], in_=wo_bf[part][:].rearrange("p n j -> p (n j)")
+            )
+            for n in range(0, n1 - n0, P):
+                wo_codes.append((words[:, n : n + P].bitcast(FP8X4), scales[:, n : n + P]))
+
+        steps = [(0, FIRST // 2), (FIRST // 2, FIRST)] + [(c, c + STEP) for c in range(FIRST, T2, STEP)]
         z_words = held([P, T2], U32, "z_words")
-        z_scales = held([P, T2], U8, "tab_rows")
-        z_names = ["z_first", "z_first", "z_third", "weights0", "weights1", "weights2"]
+        z_scales = held([P, T2], U8, "z_scales")
 
-        def chunk(c):
-            return slice(starts[c], starts[c] + CHUNKS[c])
+        def damp_step(i):
+            c0, c1 = steps[i]
+            at = AT_WO_B + (c0 * 4 if i < 2 else KB + (i - 2) % 3 * KB)
+            squares = placed([P, c1 - c0], F32, f"step_squares{i}", at)
+            nc.scalar.activation(squares[:], pages[1][:, c0:c1], ACT.Square)
+            inverse_root(PACK - 1, c0, c1, squares[:])
 
-        def halves(cols):
-            middle = (cols.start + cols.stop) // 2
-            return (slice(cols.start, middle), slice(middle, cols.stop))
-
-        def shifted(cols, first):
-            return slice(cols.start - first, cols.stop - first)
-
-        def form_z(c):
-            cols = chunk(c)
-            z_bf = held([P, CHUNKS[c], PACK], BF16, z_names[c])
-            if c < NARROW:
+        def form_z(i):
+            c0, c1 = steps[i]
+            z_bf = placed([P, c1 - c0, PACK], BF16, f"z_bf{i}", AT_ROUNDED + c0 * 8)
+            if c1 <= FIRST:
                 nc.vector.tensor_tensor(
                     z_bf[:].rearrange("p (c i) j -> p c j i", i=2),
-                    base_sb[:, :, cols].rearrange("p j (c i) -> p c j i", i=2),
-                    factors[:, :, cols].rearrange("p j (c i) -> p c j i", i=2),
+                    base_sb[:, :, c0:c1].rearrange("p j (c i) -> p c j i", i=2),
+                    first_factors[:, :, c0:c1].rearrange("p j (c i) -> p c j i", i=2),
                     MULT,
                 )
                 return z_bf
-            for part in halves(cols):
-                nc.vector.tensor_tensor(
-                    pairs[:, 1, shifted(part, wide.start), :].rearrange("p (c i) j -> p c j i", i=4),
-                    base_sb[:, 2:PACK, part].rearrange("p j (c i) -> p c j i", i=4),
-                    factors[:, 2:PACK, part].rearrange("p j (c i) -> p c j i", i=4),
-                    MULT,
-                )
+            part = slice(c0 - FIRST, c1 - FIRST)
+            nc.vector.tensor_tensor(
+                pairs[:, 1, part, :].rearrange("p (c i) j -> p c j i", i=4),
+                base_sb[:, 2:PACK, c0:c1].rearrange("p j (c i) -> p c j i", i=4),
+                late_factors[:, :, part].rearrange("p j (c i) -> p c j i", i=4),
+                MULT,
+            )
             pair_words = pairs[:].rearrange("p h c j -> p h (c j)").bitcast(I32)
-            for part in halves(cols):
-                nc.vector.tensor_copy(
-                    z_bf[:, shifted(part, cols.start), :].bitcast(I32).rearrange("p (c i) h -> p c h i", i=2),
-                    pair_words[:, :, shifted(part, wide.start)].rearrange("p h (c i) -> p c h i", i=2),
-                )
+            nc.vector.tensor_copy(
+                z_bf[:].bitcast(I32).rearrange("p (c i) h -> p c h i", i=2),
+                pair_words[:, :, part].rearrange("p h (c i) -> p c h i", i=2),
+            )
             return z_bf
 
-        def quantize_z(c, z_bf):
-            for part in (chunk(c),) if c < NARROW else halves(chunk(c)):
-                nc.vector.quantize_mx(
-                    out=z_words[:, part].bitcast(FP8X4),
-                    scales=z_scales[:, part],
-                    in_=z_bf[:, shifted(part, starts[c]), :].rearrange("p c j -> p (c j)"),
-                )
+        def quantize_z(i, z_bf):
+            c0, c1 = steps[i]
+            nc.vector.quantize_mx(
+                out=z_words[:, c0:c1].bitcast(FP8X4),
+                scales=z_scales[:, c0:c1],
+                in_=z_bf[:].rearrange("p c j -> p (c j)"),
+            )
 
+        out_rows = out.rearrange("(n p) t -> p n t", p=P)
+        starts = [sum(CHUNKS[:c]) for c in range(len(CHUNKS))]
         filled = []
 
         def project(c):
             width = CHUNKS[c]
-            per_bank = 2 if c < NARROW else 1
-            banks = N // P // per_bank
-            share = VECTOR_BANKS[c]
-            for bank in range(banks):
-                n0 = bank * per_bank
-                slot = len(filled) % STAGES
-                result = stage.tile([P, per_bank, width], F32, name=f"result{slot}", offset=slot * BANK * 4)
-                acc = psum.tile([P, per_bank, width], F32, name=f"bank{len(filled) % BANKS}")
-                filled.append(n0)
-                for i in range(per_bank):
-                    rows = slice((n0 + i) * P, (n0 + i + 1) * P)
+            cols = slice(starts[c], starts[c] + width)
+            per_bank = 2 if width < BANK else 1
+            for i in range(N // P // per_bank):
+                n0 = i * per_bank
+                at = AT_WEIGHTS + sum(filled)
+                result = placed([P, per_bank, width], F32, f"result{len(filled)}", at)
+                acc = bank(len(filled) % BANKS, [P, per_bank, width])
+                filled.append(per_bank * width * 4)
+                for n in range(per_bank):
+                    codes, scales = wo_codes[n0 + n]
                     nc.tensor.matmul_mx(
-                        out=acc[:, i, :],
-                        lhsT=wo_w[:, rows].bitcast(FP8X4),
-                        lhsT_scale=wo_s[:, rows],
-                        rhs=z_words[:, chunk(c)].bitcast(FP8X4),
-                        rhs_scale=z_scales[:, chunk(c)],
+                        out=acc[:, n, :],
+                        lhsT=codes,
+                        lhsT_scale=scales,
+                        rhs=z_words[:, cols].bitcast(FP8X4),
+                        rhs_scale=z_scales[:, cols],
                         start=True,
                         stop=True,
                     )
-                if (bank - 1) * share % banks < share:
+                if i in VECTOR_BANKS[c]:
                     nc.vector.tensor_copy(result[:], acc[:])
                 else:
                     nc.scalar.copy(result[:], acc[:])
-                nc.sync.dma_start(out_rows[:, n0 : n0 + per_bank, chunk(c)], result[:])
+                nc.sync.dma_start(out_rows[:, n0 : n0 + per_bank, cols], result[:])
 
-        for c in range(EARLY):
-            squares = placed([P, CHUNKS[c]], F32, f"early_squares{c % 2}", squares_at + c % 2 * REGION // 2)
-            damp(PACK - 1, chunk(c), squares)
-        quantize_z(0, form_z(0))
+        quantize_wo(0, AT_LAST)
+        for i in range(4):
+            damp_step(i)
+        z_bf = form_z(0)
+        quantize_wo(1, AT_WO_B - KB // 2)
+        quantize_z(0, z_bf)
+        done = 1
+        damped = 4
         for c in range(len(CHUNKS)):
-            if EARLY <= c + LAG < len(CHUNKS):
-                damp(PACK - 1, chunk(c + LAG), held([P, CHUNKS[c + LAG]], F32, z_names[c]))
-            if c + 1 < len(CHUNKS):
-                quantize_z(c + 1, form_z(c + 1))
+            ahead = starts[c + 1] + CHUNKS[c + 1] if c + 1 < len(CHUNKS) else T2
+            while done < len(steps) and steps[done][1] <= ahead:
+                while damped <= done:
+                    damp_step(damped)
+                    damped = damped + 1
+                quantize_z(done, form_z(done))
+                done = done + 1
             project(c)

@@ -25,10 +25,10 @@ BANKS = 8
 KB = 1024
 
 ZEROED = 1536
-FIRST = 256
+FIRST = 512
 REST = T2 - FIRST
 STEP = 256
-WO_SPLIT = 512
+LAG = 6
 
 CHUNKS = (128, 128, 256, 512, 512, 512)
 VECTOR_BANKS = ((), (), (), (1,), (1, 4), (1, 3, 5))
@@ -41,12 +41,12 @@ AT_WEIGHTS = 80 * KB
 AT_GATED = 96 * KB
 AT_VALUES = 102 * KB
 AT_SPARE = 116 * KB
+AT_FIRST_WEIGHTS = 124 * KB
 AT_LAST = 128 * KB
-AT_WO_A = 134 * KB
+AT_WO = 132 * KB
 AT_SQUARES = 140 * KB
-AT_WO_B = 149 * KB
-AT_ROUNDED = 157 * KB
-AT_KEYS = 165 * KB
+AT_ROUNDED = 148 * KB
+AT_KEYS = 156 * KB
 
 
 def tile_list_landmark_gated_damping_kernel(
@@ -89,18 +89,19 @@ def tile_list_landmark_gated_damping_kernel(
         nc.vector.memset(pages[1][:, 0 : ZEROED // 2 + 1], 0.0)
         nc.vector.memset(pages[1][:, ZEROED // 2 + 1 : ZEROED], 0.0)
 
-        pieces = [(0, 0, HALF), (0, HALF, S), (1, 0, HALF), (1, HALF, S), (2, 0, S), (3, 0, S)]
+        pieces = [(0, 0, HALF), (1, 0, HALF), (0, HALF, S), (1, HALF, S), (2, 0, S), (3, 0, S)]
         weights = {}
 
         def load_words(a):
             nc.sync.dma_start(tab_w[a][:], tab_words[a].rearrange("p t i -> p (t i)").bitcast(I32))
 
-        def load_wv(a):
+        def load_wv(a, j0, j1):
             rows = wv[a * P * PACK : (a + 1) * P * PACK, :]
-            nc.sync.dma_start(wv_raw[a][:], rows.rearrange("(p j) c -> p j c", j=PACK))
+            nc.sync.dma_start(wv_raw[a][:, j0:j1, :], rows.rearrange("(p j) c -> p j c", j=PACK)[:, j0:j1, :])
 
         def load_weights(t, j0, j1):
-            tile = placed([P, j1 - j0], F32, f"weights{t}_{j0}", AT_WEIGHTS + (t * S + j0) * 4)
+            at = AT_FIRST_WEIGHTS if (t, j0) == (0, 0) else AT_WEIGHTS + (t * S + j0) * 4
+            tile = placed([P, j1 - j0], F32, f"weights{t}_{j0}", at)
             rows = wgs.rearrange("(u t e) j -> t u e j", t=PACK, e=2)[t, :, :, j0:j1]
             for q in (0, 2, 1, 3):
                 nc.sync.dma_start(tile[32 * q : 32 * q + 32, :], rows)
@@ -127,15 +128,7 @@ def tile_list_landmark_gated_damping_kernel(
         def key_scales(a, s):
             return key_s[:, a, s * HALF // 4 : (s + 1) * HALF // 4].bitcast(U8)
 
-        wo_cols = ((0, WO_SPLIT), (WO_SPLIT, N))
-        wo_raw = [
-            placed([P, PACK, n1 - n0], F32, f"wo_raw{n0}", at) for (n0, n1), at in zip(wo_cols, (AT_WO_A, AT_WO_B))
-        ]
-
-        def load_wo(part):
-            n0, n1 = wo_cols[part]
-            for t in range(PACK):
-                load_plane(wo_raw[part], wo[:, n0:n1], t)
+        wo_raw = placed([P, PACK, N], F32, "wo_raw", AT_WO)
 
         nc.sync.dma_start(picks[:], offs)
         nc.sync.dma_start(tab_rows[0:32, :], tab_scales.bitcast(I32).rearrange("a q w -> q a w"))
@@ -147,22 +140,22 @@ def tile_list_landmark_gated_damping_kernel(
                 wg_scales.bitcast(I32)[:, 4 * q : 4 * q + 4, :].rearrange("a r w -> r a w"),
             )
         load_words(1)
+        load_wv(0, 0, 2)
         nc.vector.tensor_copy(picked_rows[:], tab_rows[:].bitcast(U8).indirect(picks[:]))
         for q in (0, 2, 1, 3):
             nc.sync.dma_start(key_s[32 * q : 32 * q + 4, :, :], picked_rows[:].bitcast(I32)[8 * q : 8 * q + 8, :])
-        load_wv(0)
-        load_wv(1)
+        load_wv(0, 2, PACK)
+        load_wv(1, 0, PACK)
         load_weights(0, 0, HALF)
         nc.sync.dma_start(places[:], offs2)
-        load_weights(0, HALF, S)
-        load_weights(1, 0, S)
-        load_wo(0)
+        for piece in range(1, 4):
+            load_weights(*pieces[piece])
+        for t in range(PACK):
+            load_plane(wo_raw, wo, t)
         load_weights(2, 0, S)
         load_weights(3, 0, S)
-        for t in range(PACK - 1):
+        for t in range(PACK):
             load_plane(base_sb, base, t)
-        load_wo(1)
-        load_plane(base_sb, base, PACK - 1)
 
         wg_w = [held([P, PASSES, H // 4], I32, "wg_w")]
         wg_s = held([P, PASSES, H], U8, "wg_s")
@@ -184,8 +177,8 @@ def tile_list_landmark_gated_damping_kernel(
         def round_wv(a, t0, t1, copy):
             rounded = placed([P, t1 - t0, P, PACK], BF16, f"wv_bf{a}_{t0}", AT_ROUNDED + (PACK * a + t0) * KB)
             copy(
-                rounded[:].rearrange("p t (u e) j -> p u t j e", e=2),
-                wv_raw[a][:].rearrange("p j (u t e) -> p u t j e", t=PACK, e=2)[:, :, t0:t1, :, :],
+                rounded[:].rearrange("p t (u e) j -> p u j t e", e=2),
+                wv_raw[a][:].rearrange("p j (u t e) -> p u j t e", t=PACK, e=2)[:, :, :, t0:t1, :],
             )
             return rounded
 
@@ -246,47 +239,46 @@ def tile_list_landmark_gated_damping_kernel(
         quantize_wv(0, 0, 2, rounded[0], wv_words(0, 0, 2))
         quantize_wv(0, 2, PACK, rounded[1], wv_words(0, 2, PACK))
 
-        gated = [placed([P, HALF], F32, f"gated{i}", AT_SPARE + i * 2 * KB) for i in range(4)]
-        gated.append(placed([P, S], F32, "gated4", AT_GATED + 2 * KB))
-        gated.append(placed([P, S], F32, "gated5", AT_LAST))
+        gated = [placed([P, HALF], F32, f"gated{i}", AT_SPARE + i * 2 * KB) for i in range(2)]
         values = [None] + [placed([P, HALF], F32, f"values{i}", AT_VALUES + (i - 1) * 2 * KB) for i in range(1, 4)]
         gate(0, 0, 0, gated[0][:])
-        gate(1, 0, 1, gated[2][:])
-        gate(0, 1, 2, gated[1][:])
-        early = [bank(3 + s, [P, BANK]) for s in range(2)]
-        for s in range(2):
-            value_pass(early[s], 0, s, 0, True)
+        gate(1, 0, 1, gated[1][:])
+        early = [bank(3 + t, [P, BANK]) for t in range(2)]
+        for t in range(2):
+            value_pass(early[t], t, 0, 0, True)
         rounded = [round_wv(1, t, t + 1, nc.vector.tensor_copy) for t in range(2)]
         rounded.append(round_wv(1, 2, PACK, nc.scalar.copy))
+        gated.append(placed([P, HALF], F32, "gated2", AT_WV + 14 * KB))
+        gated.append(placed([P, HALF], F32, "gated3", AT_SPARE + 4 * KB))
+        gated.append(placed([P, S], F32, "gated4", AT_GATED + 2 * KB))
+        gated.append(placed([P, S], F32, "gated5", AT_LAST))
+        gate(0, 1, 2, gated[2][:])
         for t in range(2):
             quantize_wv(1, t, t + 1, rounded[t], wv_words(1, t, t + 1))
-        for s in range(2):
-            value_pass(early[s], 0, s, 1, False)
+        for t in range(2):
+            value_pass(early[t], t, 0, 1, False)
         wg_w.append(placed([P, PASSES, H // 4], I32, "wg_late", AT_ROUNDED + PACK * KB))
         permute_wg_words(1, nc.vector.tensor_copy)
         nc.vector.tensor_tensor(gated[0][:], gated[0][:], weights_of(0, 0, HALF), MULT)
         first_h = placed([P, HALF], F32, "first_h", AT_GATED)
         nc.vector.tensor_tensor(first_h[:], early[0][:], gated[0][:], MULT)
+        quantize_wv(1, 2, PACK, rounded[2], placed([P, 2 * P], U32, "wv_late", AT_FIRST_WEIGHTS))
         scatter(0, first_h[:])
         nc.scalar.copy(values[1][:], early[1][:])
-        quantize_wv(1, 2, PACK, rounded[2], placed([P, 2 * P], U32, "wv_late", AT_SPARE))
-        value(1, 0, 5, values[2][:])
+        value(0, 1, 5, values[2][:])
         value(1, 1, 6, values[3][:])
-        gate(1, 1, 3, gated[3][:])
+        gate(1, 1, 4, gated[3][:])
         for t, gate_banks in ((2, (7, 0)), (3, (1, 2))):
             for s in range(2):
                 gate(t, s, gate_banks[s], gated[t + 2][:, s * HALF : (s + 1) * HALF])
-        def round_wo(part, rounded_wo):
-            nc.scalar.activation(
-                rounded_wo[:].rearrange("p (c i) j -> p c j i", i=2),
-                wo_raw[part][:].rearrange("p j (c i) -> p c j i", i=2),
-                ACT.Copy,
-            )
-
-        wo_bf = [held([P, WO_SPLIT, PACK], BF16, "wo_bf0")]
-        round_wo(0, wo_bf[0])
-        values.extend(placed([P, S], F32, f"values{i}", AT_WO_A + (4 * i - 18) * KB) for i in (4, 5))
-        for t, value_banks in ((2, (4, 5)), (3, (6, 7))):
+        wo_bf = held([P, N, PACK], BF16, "wo_bf")
+        nc.scalar.activation(
+            wo_bf[:].rearrange("p (c i) j -> p c j i", i=4),
+            wo_raw[:].rearrange("p j (c i) -> p c j i", i=4),
+            ACT.Copy,
+        )
+        values.extend(placed([P, S], F32, f"values{i}", AT_WO + (i - 4) * 4 * KB) for i in (4, 5))
+        for t, value_banks in ((2, (5, 6)), (3, (3, 7))):
             for s in range(2):
                 value(t, s, value_banks[s], values[t + 2][:, s * HALF : (s + 1) * HALF])
 
@@ -294,7 +286,7 @@ def tile_list_landmark_gated_damping_kernel(
             t, j0, j1 = pieces[piece]
             weighed = gated[piece]
             if piece == 1:
-                weighed = placed([P, HALF], F32, "weighed", AT_WEIGHTS)
+                weighed = placed([P, HALF], F32, "weighed", AT_FIRST_WEIGHTS + KB)
             nc.gpsimd.tensor_tensor(weighed[:], gated[piece][:], weights_of(t, j0, j1), MULT)
             nc.gpsimd.tensor_tensor(gated[piece][:], weighed[:], values[piece][:], MULT)
 
@@ -312,48 +304,38 @@ def tile_list_landmark_gated_damping_kernel(
         def inverse_root(t, c0, c1, squares):
             nc.scalar.activation(factors(t, c0, c1), squares, ACT.Abs_reciprocal_sqrt, bias=1.0)
 
-        def damp_plane(t, at):
-            squares = placed([P, T2], F32, f"squares{t}", at)
+        def damp_plane(t):
+            squares = placed([P, T2], F32, f"squares{t}", AT_SQUARES)
             nc.scalar.activation(squares[:], pages[t % 2][:], ACT.Square)
             inverse_root(t, 0, FIRST, squares[:, 0:FIRST])
             inverse_root(t, FIRST, T2, squares[:, FIRST:T2])
 
-        for piece in range(1, 4):
+        for piece in range(1, len(pieces)):
             combine(piece)
             scatter(piece, gated[piece][:])
-            if piece % 2 == 1:
-                damp_plane(piece // 2, AT_SQUARES)
-        wo_bf.append(placed([P, N - WO_SPLIT, PACK], BF16, "wo_bf1", AT_SQUARES))
-        round_wo(1, wo_bf[1])
-        combine(4)
-        scatter(4, gated[4][:])
-        damp_plane(2, AT_WO_B)
-        combine(5)
-        scatter(5, gated[5][:])
+            if 2 <= piece < len(pieces) - 1:
+                damp_plane(piece - 2)
 
         pairs = held([P, 2, REST, 2], BF16, "pairs")
         for t in range(2):
             nc.gpsimd.tensor_tensor(pairs[:, 0, :, t], base_sb[:, t, FIRST:T2], early_factors[t][:], MULT)
 
-        wo_codes = []
-
-        def quantize_wo(part, at):
-            n0, n1 = wo_cols[part]
-            words = placed([P, n1 - n0], U32, f"wo_w{part}", at)
-            scales = held([P, n1 - n0], U8, f"wo_s{part}")
+        wo_w = placed([P, N], U32, "wo_w", AT_LAST)
+        wo_s = held([P, N], U8, "wo_s")
+        for n0, n1 in ((0, BANK), (BANK, N)):
             nc.vector.quantize_mx(
-                out=words[:].bitcast(FP8X4), scales=scales[:], in_=wo_bf[part][:].rearrange("p n j -> p (n j)")
+                out=wo_w[:, n0:n1].bitcast(FP8X4),
+                scales=wo_s[:, n0:n1],
+                in_=wo_bf[:, n0:n1, :].rearrange("p n j -> p (n j)"),
             )
-            for n in range(0, n1 - n0, P):
-                wo_codes.append((words[:, n : n + P].bitcast(FP8X4), scales[:, n : n + P]))
 
-        steps = [(0, FIRST // 2), (FIRST // 2, FIRST)] + [(c, c + STEP) for c in range(FIRST, T2, STEP)]
+        steps = [(0, STEP // 2), (STEP // 2, STEP)] + [(c, c + STEP) for c in range(STEP, T2, STEP)]
         z_words = held([P, T2], U32, "z_words")
         z_scales = held([P, T2], U8, "z_scales")
 
         def damp_step(i):
             c0, c1 = steps[i]
-            at = AT_WO_B + (c0 * 4 if i < 2 else KB + (i - 2) % 3 * KB)
+            at = AT_SQUARES + c0 * 4 if i < LAG else AT_ROUNDED + steps[i - LAG][0] * 8
             squares = placed([P, c1 - c0], F32, f"step_squares{i}", at)
             nc.scalar.activation(squares[:], pages[1][:, c0:c1], ACT.Square)
             inverse_root(PACK - 1, c0, c1, squares[:])
@@ -406,11 +388,11 @@ def tile_list_landmark_gated_damping_kernel(
                 acc = bank(len(filled) % BANKS, [P, per_bank, width])
                 filled.append(per_bank * width * 4)
                 for n in range(per_bank):
-                    codes, scales = wo_codes[n0 + n]
+                    rows = slice((n0 + n) * P, (n0 + n + 1) * P)
                     nc.tensor.matmul_mx(
                         out=acc[:, n, :],
-                        lhsT=codes,
-                        lhsT_scale=scales,
+                        lhsT=wo_w[:, rows].bitcast(FP8X4),
+                        lhsT_scale=wo_s[:, rows],
                         rhs=z_words[:, cols].bitcast(FP8X4),
                         rhs_scale=z_scales[:, cols],
                         start=True,
@@ -422,12 +404,9 @@ def tile_list_landmark_gated_damping_kernel(
                     nc.scalar.copy(result[:], acc[:])
                 nc.sync.dma_start(out_rows[:, n0 : n0 + per_bank, cols], result[:])
 
-        quantize_wo(0, AT_LAST)
         for i in range(4):
             damp_step(i)
-        z_bf = form_z(0)
-        quantize_wo(1, AT_WO_B - KB // 2)
-        quantize_z(0, z_bf)
+        quantize_z(0, form_z(0))
         done = 1
         damped = 4
         for c in range(len(CHUNKS)):

@@ -28,10 +28,11 @@ ZEROED = 1536
 FIRST = 512
 REST = T2 - FIRST
 STEP = 256
-LAG = 6
+AT_ONCE = 6
+LAG = 7
 
 CHUNKS = (128, 128, 256, 512, 512, 512)
-VECTOR_BANKS = ((), (), (), (1,), (1, 4), (1, 3, 5))
+VECTOR_BANKS = ((), (), (), (1, 4), (1,), (1, 3, 5))
 
 AT_TAB = 0
 AT_WV = 16 * KB
@@ -47,6 +48,7 @@ AT_WO = 132 * KB
 AT_SQUARES = 140 * KB
 AT_ROUNDED = 148 * KB
 AT_KEYS = 156 * KB
+AT_FIRST_Z = 164 * KB
 
 
 def tile_list_landmark_gated_damping_kernel(
@@ -128,7 +130,13 @@ def tile_list_landmark_gated_damping_kernel(
         def key_scales(a, s):
             return key_s[:, a, s * HALF // 4 : (s + 1) * HALF // 4].bitcast(U8)
 
-        wo_raw = placed([P, PACK, N], F32, "wo_raw", AT_WO)
+        wo_cols = ((0, BANK), (BANK, N))
+        wo_raw = [placed([P, PACK, n1 - n0], F32, f"wo_raw{n0}", AT_WO + n0 * 16) for n0, n1 in wo_cols]
+
+        def load_wo(part):
+            n0, n1 = wo_cols[part]
+            for t in range(PACK):
+                load_plane(wo_raw[part], wo[:, n0:n1], t)
 
         nc.sync.dma_start(picks[:], offs)
         nc.sync.dma_start(tab_rows[0:32, :], tab_scales.bitcast(I32).rearrange("a q w -> q a w"))
@@ -150,9 +158,9 @@ def tile_list_landmark_gated_damping_kernel(
         nc.sync.dma_start(places[:], offs2)
         for piece in range(1, 4):
             load_weights(*pieces[piece])
-        for t in range(PACK):
-            load_plane(wo_raw, wo, t)
+        load_wo(0)
         load_weights(2, 0, S)
+        load_wo(1)
         load_weights(3, 0, S)
         for t in range(PACK):
             load_plane(base_sb, base, t)
@@ -271,16 +279,18 @@ def tile_list_landmark_gated_damping_kernel(
         for t, gate_banks in ((2, (7, 0)), (3, (1, 2))):
             for s in range(2):
                 gate(t, s, gate_banks[s], gated[t + 2][:, s * HALF : (s + 1) * HALF])
-        wo_bf = held([P, N, PACK], BF16, "wo_bf")
-        nc.scalar.activation(
-            wo_bf[:].rearrange("p (c i) j -> p c j i", i=4),
-            wo_raw[:].rearrange("p j (c i) -> p c j i", i=4),
-            ACT.Copy,
-        )
-        values.extend(placed([P, S], F32, f"values{i}", AT_WO + (i - 4) * 4 * KB) for i in (4, 5))
+        values.extend(placed([P, S], F32, f"values{i}", AT_VALUES + (4 * i - 10) * KB) for i in (4, 5))
         for t, value_banks in ((2, (5, 6)), (3, (3, 7))):
             for s in range(2):
                 value(t, s, value_banks[s], values[t + 2][:, s * HALF : (s + 1) * HALF])
+
+        wo_bf = held([P, N, PACK], BF16, "wo_bf")
+        for part, (n0, n1) in enumerate(wo_cols):
+            nc.scalar.activation(
+                wo_bf[:, n0:n1, :].rearrange("p (c i) j -> p c j i", i=4),
+                wo_raw[part][:].rearrange("p j (c i) -> p c j i", i=4),
+                ACT.Copy,
+            )
 
         def combine(piece):
             t, j0, j1 = pieces[piece]
@@ -322,27 +332,31 @@ def tile_list_landmark_gated_damping_kernel(
 
         wo_w = placed([P, N], U32, "wo_w", AT_LAST)
         wo_s = held([P, N], U8, "wo_s")
-        for n0, n1 in ((0, BANK), (BANK, N)):
+        for n0, n1 in wo_cols:
             nc.vector.quantize_mx(
                 out=wo_w[:, n0:n1].bitcast(FP8X4),
                 scales=wo_s[:, n0:n1],
                 in_=wo_bf[:, n0:n1, :].rearrange("p n j -> p (n j)"),
             )
 
-        steps = [(0, STEP // 2), (STEP // 2, STEP)] + [(c, c + STEP) for c in range(STEP, T2, STEP)]
+        steps = [(c, c + STEP // 2) for c in range(0, FIRST, STEP // 2)]
+        steps.extend((c, c + STEP) for c in range(FIRST, T2, STEP))
         z_words = held([P, T2], U32, "z_words")
         z_scales = held([P, T2], U8, "z_scales")
 
+        def z_at(i):
+            return AT_FIRST_Z + KB + i * KB if i <= 0 else AT_ROUNDED + steps[i][0] * 8
+
         def damp_step(i):
             c0, c1 = steps[i]
-            at = AT_SQUARES + c0 * 4 if i < LAG else AT_ROUNDED + steps[i - LAG][0] * 8
+            at = AT_SQUARES + c0 * 4 if i < AT_ONCE else z_at(i - LAG) + (KB // 2 if i <= LAG else 0)
             squares = placed([P, c1 - c0], F32, f"step_squares{i}", at)
             nc.scalar.activation(squares[:], pages[1][:, c0:c1], ACT.Square)
             inverse_root(PACK - 1, c0, c1, squares[:])
 
         def form_z(i):
             c0, c1 = steps[i]
-            z_bf = placed([P, c1 - c0, PACK], BF16, f"z_bf{i}", AT_ROUNDED + c0 * 8)
+            z_bf = placed([P, c1 - c0, PACK], BF16, f"z_bf{i}", z_at(i))
             if c1 <= FIRST:
                 nc.vector.tensor_tensor(
                     z_bf[:].rearrange("p (c i) j -> p c j i", i=2),

@@ -165,20 +165,16 @@ def tile_list_landmark_gated_damping_kernel(
         for t in range(PACK):
             load_plane(base_sb, base, t)
 
-        wg_w = [held([P, PASSES, H // 4], I32, "wg_w")]
+        wg_w = held([P, PASSES, H // 2], I32, "wg_w")
         wg_s = held([P, PASSES, H], U8, "wg_s")
         nc.gpsimd.tensor_copy(
             wg_s[:].rearrange("p a (t u e) -> p a t u e", t=PACK, e=2),
             wg_raw_s[:].bitcast(U8).rearrange("p a (u t e) -> p a t u e", t=PACK, e=2),
         )
-
-        def permute_wg_words(half, copy):
-            copy(
-                wg_w[half][:].rearrange("p a (t u) -> p a t u", t=2),
-                wg_raw_w[:].rearrange("p a (u t) -> p a t u", t=PACK)[:, :, 2 * half : 2 * half + 2, :],
-            )
-
-        permute_wg_words(0, nc.gpsimd.tensor_copy)
+        nc.gpsimd.tensor_copy(
+            wg_w[:].rearrange("p a (t u) -> p a t u", t=PACK),
+            wg_raw_w[:].rearrange("p a (u t) -> p a t u", t=PACK),
+        )
 
         wv_codes = {}
 
@@ -208,7 +204,7 @@ def tile_list_landmark_gated_damping_kernel(
             for a in order:
                 nc.tensor.matmul_mx(
                     out=acc[:],
-                    lhsT=wg_w[t // 2][:, a, t % 2 * P // 2 : (t % 2 + 1) * P // 2].bitcast(FP4X4),
+                    lhsT=wg_w[:, a, t * P // 2 : (t + 1) * P // 2].bitcast(FP4X4),
                     lhsT_scale=wg_s[:, a, t * P : (t + 1) * P],
                     rhs=key_w[a][s][:].bitcast(FP8X4),
                     rhs_scale=key_scales(a, s),
@@ -243,11 +239,13 @@ def tile_list_landmark_gated_damping_kernel(
         gather_words(0, 1)
         gather_words(1, 0)
         gather_words(1, 1)
-        rounded = [round_wv(0, t, t + 2, nc.vector.tensor_copy) for t in (0, 2)]
+        warm = held([P, 8], F32, "warm")
+        nc.scalar.activation(warm[:, 0:1], pages[1][:, 0:1], ACT.Sigmoid)
+        rounded = [round_wv(0, 0, 2, nc.vector.tensor_copy), round_wv(0, 2, PACK, nc.scalar.copy)]
         quantize_wv(0, 0, 2, rounded[0], wv_words(0, 0, 2))
         quantize_wv(0, 2, PACK, rounded[1], wv_words(0, 2, PACK))
 
-        gated = [placed([P, HALF], F32, f"gated{i}", AT_SPARE + i * 2 * KB) for i in range(2)]
+        gated = [placed([P, HALF], F32, f"gated{i}", AT_WV + i * 2 * KB) for i in range(2)]
         values = [None] + [placed([P, HALF], F32, f"values{i}", AT_VALUES + (i - 1) * 2 * KB) for i in range(1, 4)]
         gate(0, 0, 0, gated[0][:])
         gate(1, 0, 1, gated[1][:])
@@ -265,22 +263,20 @@ def tile_list_landmark_gated_damping_kernel(
             quantize_wv(1, t, t + 1, rounded[t], wv_words(1, t, t + 1))
         for t in range(2):
             value_pass(early[t], t, 0, 1, False)
-        wg_w.append(placed([P, PASSES, H // 4], I32, "wg_late", AT_ROUNDED + PACK * KB))
-        permute_wg_words(1, nc.vector.tensor_copy)
         nc.vector.tensor_tensor(gated[0][:], gated[0][:], weights_of(0, 0, HALF), MULT)
         first_h = placed([P, HALF], F32, "first_h", AT_GATED)
         nc.vector.tensor_tensor(first_h[:], early[0][:], gated[0][:], MULT)
         quantize_wv(1, 2, PACK, rounded[2], placed([P, 2 * P], U32, "wv_late", AT_FIRST_WEIGHTS))
         scatter(0, first_h[:])
         nc.scalar.copy(values[1][:], early[1][:])
-        value(0, 1, 5, values[2][:])
-        value(1, 1, 6, values[3][:])
+        value(0, 1, 0, values[2][:])
+        value(1, 1, 1, values[3][:])
         gate(1, 1, 4, gated[3][:])
-        for t, gate_banks in ((2, (7, 0)), (3, (1, 2))):
+        for t, gate_banks in ((2, (2, 0)), (3, (1, 3))):
             for s in range(2):
                 gate(t, s, gate_banks[s], gated[t + 2][:, s * HALF : (s + 1) * HALF])
         values.extend(placed([P, S], F32, f"values{i}", AT_VALUES + (4 * i - 10) * KB) for i in (4, 5))
-        for t, value_banks in ((2, (5, 6)), (3, (3, 7))):
+        for t, value_banks in ((2, (5, 6)), (3, (7, 2))):
             for s in range(2):
                 value(t, s, value_banks[s], values[t + 2][:, s * HALF : (s + 1) * HALF])
 

@@ -97,9 +97,9 @@ def tile_list_landmark_gated_damping_kernel(
         def load_words(a):
             nc.sync.dma_start(tab_w[a][:], tab_words[a].rearrange("p t i -> p (t i)").bitcast(I32))
 
-        def load_wv(a, j0, j1):
+        def load_wv(a):
             rows = wv[a * P * PACK : (a + 1) * P * PACK, :]
-            nc.sync.dma_start(wv_raw[a][:, j0:j1, :], rows.rearrange("(p j) c -> p j c", j=PACK)[:, j0:j1, :])
+            nc.sync.dma_start(wv_raw[a][:], rows.rearrange("(p j) c -> p j c", j=PACK))
 
         def load_weights(t, j0, j1):
             at = AT_FIRST_WEIGHTS if (t, j0) == (0, 0) else AT_WEIGHTS + (t * S + j0) * 4
@@ -148,12 +148,11 @@ def tile_list_landmark_gated_damping_kernel(
                 wg_scales.bitcast(I32)[:, 4 * q : 4 * q + 4, :].rearrange("a r w -> r a w"),
             )
         load_words(1)
-        load_wv(0, 0, 2)
+        load_wv(0)
         nc.vector.tensor_copy(picked_rows[:], tab_rows[:].bitcast(U8).indirect(picks[:]))
         for q in (0, 2, 1, 3):
             nc.sync.dma_start(key_s[32 * q : 32 * q + 4, :, :], picked_rows[:].bitcast(I32)[8 * q : 8 * q + 8, :])
-        load_wv(0, 2, PACK)
-        load_wv(1, 0, PACK)
+        load_wv(1)
         load_weights(0, 0, HALF)
         nc.sync.dma_start(places[:], offs2)
         for piece in range(1, 4):
@@ -239,13 +238,11 @@ def tile_list_landmark_gated_damping_kernel(
         gather_words(0, 1)
         gather_words(1, 0)
         gather_words(1, 1)
-        warm = held([P, 8], F32, "warm")
-        nc.scalar.activation(warm[:, 0:1], pages[1][:, 0:1], ACT.Sigmoid)
-        rounded = [round_wv(0, 0, 2, nc.vector.tensor_copy), round_wv(0, 2, PACK, nc.scalar.copy)]
+        rounded = [round_wv(0, t, t + 2, nc.vector.tensor_copy) for t in (0, 2)]
         quantize_wv(0, 0, 2, rounded[0], wv_words(0, 0, 2))
         quantize_wv(0, 2, PACK, rounded[1], wv_words(0, 2, PACK))
 
-        gated = [placed([P, HALF], F32, f"gated{i}", AT_WV + i * 2 * KB) for i in range(2)]
+        gated = [placed([P, HALF], F32, f"gated{i}", AT_SPARE + i * 2 * KB) for i in range(2)]
         values = [None] + [placed([P, HALF], F32, f"values{i}", AT_VALUES + (i - 1) * 2 * KB) for i in range(1, 4)]
         gate(0, 0, 0, gated[0][:])
         gate(1, 0, 1, gated[1][:])
@@ -254,11 +251,9 @@ def tile_list_landmark_gated_damping_kernel(
             value_pass(early[t], t, 0, 0, True)
         rounded = [round_wv(1, t, t + 1, nc.vector.tensor_copy) for t in range(2)]
         rounded.append(round_wv(1, 2, PACK, nc.scalar.copy))
-        gated.append(placed([P, HALF], F32, "gated2", AT_WV + 14 * KB))
-        gated.append(placed([P, HALF], F32, "gated3", AT_SPARE + 4 * KB))
+        gated.extend(placed([P, HALF], F32, f"gated{i}", AT_SPARE + i * 2 * KB) for i in (2, 3))
         gated.append(placed([P, S], F32, "gated4", AT_GATED + 2 * KB))
         gated.append(placed([P, S], F32, "gated5", AT_LAST))
-        gate(0, 1, 2, gated[2][:])
         for t in range(2):
             quantize_wv(1, t, t + 1, rounded[t], wv_words(1, t, t + 1))
         for t in range(2):
@@ -271,8 +266,9 @@ def tile_list_landmark_gated_damping_kernel(
         nc.scalar.copy(values[1][:], early[1][:])
         value(0, 1, 0, values[2][:])
         value(1, 1, 1, values[3][:])
-        gate(1, 1, 4, gated[3][:])
-        for t, gate_banks in ((2, (2, 0)), (3, (1, 3))):
+        gate(0, 1, 4, gated[2][:])
+        gate(1, 1, 1, gated[3][:])
+        for t, gate_banks in ((2, (0, 3)), (3, (4, 0))):
             for s in range(2):
                 gate(t, s, gate_banks[s], gated[t + 2][:, s * HALF : (s + 1) * HALF])
         values.extend(placed([P, S], F32, f"values{i}", AT_VALUES + (4 * i - 10) * KB) for i in (4, 5))

@@ -25,14 +25,13 @@ BANKS = 8
 KB = 1024
 
 ZEROED = 1536
-FIRST = 512
-REST = T2 - FIRST
+PAIRED = 1536
 STEP = 256
 AT_ONCE = 6
 LAG = 7
 
 CHUNKS = (128, 128, 256, 512, 512, 512)
-VECTOR_BANKS = ((), (), (), (1, 4), (1,), (1, 3, 5))
+VECTOR_BANKS = ((), (), (1,), (1, 4), (), (1, 3, 5))
 
 AT_TAB = 0
 AT_WV = 16 * KB
@@ -292,16 +291,16 @@ def tile_list_landmark_gated_damping_kernel(
             nc.gpsimd.tensor_tensor(weighed[:], gated[piece][:], weights_of(t, j0, j1), MULT)
             nc.gpsimd.tensor_tensor(gated[piece][:], weighed[:], values[piece][:], MULT)
 
-        first_factors = held([P, PACK, FIRST], F32, "first_factors")
-        early_factors = [placed([P, REST], F32, f"factors{t}", AT_TAB + t * 8 * KB) for t in range(2)]
-        late_factors = placed([P, 2, REST], F32, "late_factors", AT_WV)
+        early_factors = [placed([P, PAIRED], F32, f"factors{t}", AT_TAB + t * 8 * KB) for t in range(2)]
+        late_factors = placed([P, 2, PAIRED], F32, "late_factors", AT_WV)
+        last_factors = held([P, PACK, T2 - PAIRED], F32, "last_factors")
 
         def factors(t, c0, c1):
-            if c1 <= FIRST:
-                return first_factors[:, t, c0:c1]
+            if c0 >= PAIRED:
+                return last_factors[:, t, c0 - PAIRED : c1 - PAIRED]
             if t < 2:
-                return early_factors[t][:, c0 - FIRST : c1 - FIRST]
-            return late_factors[:, t - 2, c0 - FIRST : c1 - FIRST]
+                return early_factors[t][:, c0:c1]
+            return late_factors[:, t - 2, c0:c1]
 
         def inverse_root(t, c0, c1, squares):
             nc.scalar.activation(factors(t, c0, c1), squares, ACT.Abs_reciprocal_sqrt, bias=1.0)
@@ -309,8 +308,8 @@ def tile_list_landmark_gated_damping_kernel(
         def damp_plane(t):
             squares = placed([P, T2], F32, f"squares{t}", AT_SQUARES)
             nc.scalar.activation(squares[:], pages[t % 2][:], ACT.Square)
-            inverse_root(t, 0, FIRST, squares[:, 0:FIRST])
-            inverse_root(t, FIRST, T2, squares[:, FIRST:T2])
+            inverse_root(t, 0, PAIRED, squares[:, 0:PAIRED])
+            inverse_root(t, PAIRED, T2, squares[:, PAIRED:T2])
 
         for piece in range(1, len(pieces)):
             combine(piece)
@@ -318,9 +317,9 @@ def tile_list_landmark_gated_damping_kernel(
             if 2 <= piece < len(pieces) - 1:
                 damp_plane(piece - 2)
 
-        pairs = held([P, 2, REST, 2], BF16, "pairs")
+        pairs = held([P, 2, PAIRED, 2], BF16, "pairs")
         for t in range(2):
-            nc.gpsimd.tensor_tensor(pairs[:, 0, :, t], base_sb[:, t, FIRST:T2], early_factors[t][:], MULT)
+            nc.gpsimd.tensor_tensor(pairs[:, 0, :, t], base_sb[:, t, 0:PAIRED], early_factors[t][:], MULT)
 
         wo_w = placed([P, N], U32, "wo_w", AT_LAST)
         wo_s = held([P, N], U8, "wo_s")
@@ -331,8 +330,8 @@ def tile_list_landmark_gated_damping_kernel(
                 in_=wo_bf[:, n0:n1, :].rearrange("p n j -> p (n j)"),
             )
 
-        steps = [(c, c + STEP // 2) for c in range(0, FIRST, STEP // 2)]
-        steps.extend((c, c + STEP) for c in range(FIRST, T2, STEP))
+        steps = [(c, c + STEP // 2) for c in range(0, BANK, STEP // 2)]
+        steps.extend((c, c + STEP) for c in range(BANK, T2, STEP))
         z_words = held([P, T2], U32, "z_words")
         z_scales = held([P, T2], U8, "z_scales")
 
@@ -349,15 +348,15 @@ def tile_list_landmark_gated_damping_kernel(
         def form_z(i):
             c0, c1 = steps[i]
             z_bf = placed([P, c1 - c0, PACK], BF16, f"z_bf{i}", z_at(i))
-            if c1 <= FIRST:
+            if c0 >= PAIRED:
                 nc.vector.tensor_tensor(
                     z_bf[:].rearrange("p (c i) j -> p c j i", i=2),
                     base_sb[:, :, c0:c1].rearrange("p j (c i) -> p c j i", i=2),
-                    first_factors[:, :, c0:c1].rearrange("p j (c i) -> p c j i", i=2),
+                    last_factors[:, :, c0 - PAIRED : c1 - PAIRED].rearrange("p j (c i) -> p c j i", i=2),
                     MULT,
                 )
                 return z_bf
-            part = slice(c0 - FIRST, c1 - FIRST)
+            part = slice(c0, c1)
             nc.vector.tensor_tensor(
                 pairs[:, 1, part, :].rearrange("p (c i) j -> p c j i", i=4),
                 base_sb[:, 2:PACK, c0:c1].rearrange("p j (c i) -> p c j i", i=4),

@@ -25,7 +25,7 @@ BANKS = 8
 KB = 1024
 
 ZEROED = 1536
-PAIRED = 1536
+PAIRED = 1280
 STEP = 256
 AT_ONCE = 6
 LAG = 7

@@ -96,9 +96,9 @@ def tile_list_landmark_gated_damping_kernel(
         def load_words(a):
             nc.sync.dma_start(tab_w[a][:], tab_words[a].rearrange("p t i -> p (t i)").bitcast(I32))
 
-        def load_wv(a):
+        def load_wv(a, j0, j1):
             rows = wv[a * P * PACK : (a + 1) * P * PACK, :]
-            nc.sync.dma_start(wv_raw[a][:], rows.rearrange("(p j) c -> p j c", j=PACK))
+            nc.sync.dma_start(wv_raw[a][:, j0:j1, :], rows.rearrange("(p j) c -> p j c", j=PACK)[:, j0:j1, :])
 
         def load_weights(t, j0, j1):
             at = AT_FIRST_WEIGHTS if (t, j0) == (0, 0) else AT_WEIGHTS + (t * S + j0) * 4
@@ -147,11 +147,12 @@ def tile_list_landmark_gated_damping_kernel(
                 wg_scales.bitcast(I32)[:, 4 * q : 4 * q + 4, :].rearrange("a r w -> r a w"),
             )
         load_words(1)
-        load_wv(0)
+        load_wv(0, 0, 2)
         nc.vector.tensor_copy(picked_rows[:], tab_rows[:].bitcast(U8).indirect(picks[:]))
         for q in (0, 2, 1, 3):
             nc.sync.dma_start(key_s[32 * q : 32 * q + 4, :, :], picked_rows[:].bitcast(I32)[8 * q : 8 * q + 8, :])
-        load_wv(1)
+        load_wv(0, 2, PACK)
+        load_wv(1, 0, PACK)
         load_weights(0, 0, HALF)
         nc.sync.dma_start(places[:], offs2)
         for piece in range(1, 4):
@@ -250,9 +251,11 @@ def tile_list_landmark_gated_damping_kernel(
             value_pass(early[t], t, 0, 0, True)
         rounded = [round_wv(1, t, t + 1, nc.vector.tensor_copy) for t in range(2)]
         rounded.append(round_wv(1, 2, PACK, nc.scalar.copy))
-        gated.extend(placed([P, HALF], F32, f"gated{i}", AT_SPARE + i * 2 * KB) for i in (2, 3))
+        gated.append(placed([P, HALF], F32, "gated2", AT_WV + 14 * KB))
+        gated.append(placed([P, HALF], F32, "gated3", AT_SPARE + 4 * KB))
         gated.append(placed([P, S], F32, "gated4", AT_GATED + 2 * KB))
         gated.append(placed([P, S], F32, "gated5", AT_LAST))
+        gate(0, 1, 2, gated[2][:])
         for t in range(2):
             quantize_wv(1, t, t + 1, rounded[t], wv_words(1, t, t + 1))
         for t in range(2):
@@ -265,9 +268,8 @@ def tile_list_landmark_gated_damping_kernel(
         nc.scalar.copy(values[1][:], early[1][:])
         value(0, 1, 0, values[2][:])
         value(1, 1, 1, values[3][:])
-        gate(0, 1, 4, gated[2][:])
-        gate(1, 1, 1, gated[3][:])
-        for t, gate_banks in ((2, (0, 3)), (3, (4, 0))):
+        gate(1, 1, 4, gated[3][:])
+        for t, gate_banks in ((2, (2, 0)), (3, (1, 3))):
             for s in range(2):
                 gate(t, s, gate_banks[s], gated[t + 2][:, s * HALF : (s + 1) * HALF])
         values.extend(placed([P, S], F32, f"values{i}", AT_VALUES + (4 * i - 10) * KB) for i in (4, 5))

@@ -260,9 +260,12 @@ def tile_list_landmark_gated_damping_kernel(
             quantize_wv(1, t, t + 1, rounded[t], wv_words(1, t, t + 1))
         for t in range(2):
             value_pass(early[t], t, 0, 1, False)
-        nc.vector.tensor_tensor(gated[0][:], gated[0][:], weights_of(0, 0, HALF), MULT)
+        halves = (slice(0, HALF // 2), slice(HALF // 2, HALF))
+        for half in halves:
+            nc.vector.tensor_tensor(gated[0][:, half], gated[0][:, half], weights_of(0, 0, HALF)[:, half], MULT)
         first_h = placed([P, HALF], F32, "first_h", AT_GATED)
-        nc.vector.tensor_tensor(first_h[:], early[0][:], gated[0][:], MULT)
+        for half in halves:
+            nc.vector.tensor_tensor(first_h[:, half], early[0][:, half], gated[0][:, half], MULT)
         quantize_wv(1, 2, PACK, rounded[2], placed([P, 2 * P], U32, "wv_late", AT_FIRST_WEIGHTS))
         scatter(0, first_h[:])
         nc.scalar.copy(values[1][:], early[1][:])

@@ -393,8 +393,11 @@ def tile_list_landmark_gated_damping_kernel(
             per_bank = 2 if width < BANK else 1
             for i in range(N // P // per_bank):
                 n0 = i * per_bank
-                at = AT_WEIGHTS + sum(filled)
-                result = placed([P, per_bank, width], F32, f"result{len(filled)}", at)
+                joined = 2 if per_bank == 1 and (c, i) < (len(CHUNKS) - 1, 4) else 1
+                if i % joined == 0:
+                    at = AT_WEIGHTS + sum(filled)
+                    staged = placed([P, joined * per_bank, width], F32, f"result{len(filled)}", at)
+                result = staged[:, (i % joined) * per_bank : (i % joined + 1) * per_bank, :]
                 acc = bank(len(filled) % BANKS, [P, per_bank, width])
                 filled.append(per_bank * width * 4)
                 for n in range(per_bank):
@@ -409,10 +412,12 @@ def tile_list_landmark_gated_damping_kernel(
                         stop=True,
                     )
                 if i in VECTOR_BANKS[c]:
-                    nc.vector.tensor_copy(result[:], acc[:])
+                    nc.vector.tensor_copy(result, acc[:])
                 else:
-                    nc.scalar.copy(result[:], acc[:])
-                nc.sync.dma_start(out_rows[:, n0 : n0 + per_bank, cols], result[:])
+                    nc.scalar.copy(result, acc[:])
+                if i % joined == joined - 1:
+                    first = n0 - (joined - 1) * per_bank
+                    nc.sync.dma_start(out_rows[:, first : n0 + per_bank, cols], staged[:])
 
         for i in range(4):
             damp_step(i)

from contextlib import ExitStack

import concourse.mybir as mybir

K, H, N, T, S, T2 = 1024, 512, 768, 2048, 1024, 2048
FLOPS = 2 * (2 * K * H * S + H * N * T2)

F32 = mybir.dt.float32
BF16 = mybir.dt.bfloat16
I32 = mybir.dt.int32
U32 = mybir.dt.uint32
U16 = mybir.dt.uint16
U8 = mybir.dt.uint8
FP8X4 = mybir.dt.float8_e4m3fn_x4
FP4X4 = mybir.dt.float4_e2m1fn_x4
ACT = mybir.ActivationFunctionType
MULT = mybir.AluOpType.mult

P = 128
PACK = 4
PASSES = K // (P * PACK)
HALF = S // 2
BANK = 512
BANKS = 8
KB = 1024

ZEROED = 1536
PAIRED = 1280
STEP = 256
AT_ONCE = 6
LAG = 7

CHUNKS = (128, 128, 256, 512, 512, 512)
VECTOR_BANKS = ((), (), (1,), (1, 4), (), (1, 3, 5))

AT_TAB = 0
AT_WV = 16 * KB
AT_BASE = 32 * KB
AT_PAGES = 64 * KB
AT_WEIGHTS = 80 * KB
AT_GATED = 96 * KB
AT_VALUES = 102 * KB
AT_SPARE = 116 * KB
AT_FIRST_WEIGHTS = 124 * KB
AT_LAST = 128 * KB
AT_WO = 132 * KB
AT_SQUARES = 140 * KB
AT_ROUNDED = 148 * KB
AT_KEYS = 156 * KB
AT_FIRST_Z = 164 * KB


def tile_list_landmark_gated_damping_kernel(
    tc, tab_words, tab_scales, offs, wv, wg_words, wg_scales, offs2, wgs, base, wo, out
):
    nc = tc.nc
    with ExitStack() as ctx:
        lists = ctx.enter_context(tc.tile_pool(name="lists", bufs=1))
        shared = ctx.enter_context(tc.tile_pool(name="shared", bufs=1))
        keep = ctx.enter_context(tc.tile_pool(name="keep", bufs=1))
        psum = ctx.enter_context(tc.psum_pool(name="psum", bufs=1))

        def held(shape, dtype, name):
            return keep.tile(shape, dtype, name=name, align_bytes=64)

        def placed(shape, dtype, name, offset):
            return shared.tile(shape, dtype, name=name, align_bytes=64, offset=offset)

        def bank(i, shape):
            return psum.tile(shape, F32, name=f"bank{i}")

        picks = lists.tile([P, S // 16], U16, name="picks")
        places = lists.tile([P, S // 16], U16, name="places")

        tab_w = [placed([P, T], I32, f"tab_w{a}", AT_TAB + a * 8 * KB) for a in range(PASSES)]
        wv_raw = [placed([P, PACK, H], F32, f"wv_raw{a}", AT_WV + a * 8 * KB) for a in range(PASSES)]
        base_sb = placed([P, PACK, T2], F32, "base_sb", AT_BASE)
        pages = [placed([P, T2], F32, f"page{i}", AT_PAGES + i * 8 * KB) for i in range(2)]
        tab_rows = held([P, T // 4], I32, "tab_rows")
        key_s = held([P, PASSES, S // 4], I32, "key_s")
        wg_raw_w = held([P, PASSES, H // 2], I32, "wg_raw_w")
        wg_raw_s = held([P, PASSES, H // 4], I32, "wg_raw_s")

        nc.gpsimd.memset(wg_raw_s[:], 0)
        nc.gpsimd.memset(tab_rows[32:64, :], 0)
        nc.gpsimd.memset(tab_rows[64:128, :], 0)
        nc.gpsimd.memset(key_s[:], 0)
        nc.gpsimd.memset(pages[0][:], 0.0)
        nc.gpsimd.memset(pages[1][:, ZEROED:T2], 0.0)
        nc.vector.memset(pages[1][:, 0 : ZEROED // 2 + 1], 0.0)
        nc.vector.memset(pages[1][:, ZEROED // 2 + 1 : ZEROED], 0.0)

        pieces = [(0, 0, HALF), (1, 0, HALF), (0, HALF, S), (1, HALF, S), (2, 0, S), (3, 0, S)]
        weights = {}

        def load_words(a):
            nc.sync.dma_start(tab_w[a][:], tab_words[a].rearrange("p t i -> p (t i)").bitcast(I32))

        def load_wv(a, j0, j1):
            rows = wv[a * P * PACK : (a + 1) * P * PACK, :]
            nc.sync.dma_start(wv_raw[a][:, j0:j1, :], rows.rearrange("(p j) c -> p j c", j=PACK)[:, j0:j1, :])

        def load_weights(t, j0, j1):
            at = AT_FIRST_WEIGHTS if (t, j0) == (0, 0) else AT_WEIGHTS + (t * S + j0) * 4
            tile = placed([P, j1 - j0], F32, f"weights{t}_{j0}", at)
            rows = wgs.rearrange("(u t e) j -> t u e j", t=PACK, e=2)[t, :, :, j0:j1]
            for q in (0, 2, 1, 3):
                nc.sync.dma_start(tile[32 * q : 32 * q + 32, :], rows)
            for j in range(j0, j1, HALF):
                weights[t, j] = (tile, j - j0)

        def weights_of(t, j0, j1):
            tile, first = weights[t, j0]
            return tile[:, first : first + j1 - j0]

        def load_plane(tile, source, t):
            nc.sync.dma_start(tile[:, t, :], source.rearrange("(u t e) c -> t u e c", t=PACK, e=2)[t])

        key_w = [
            [placed([P, HALF], U32, f"key_w{a}_{s}", AT_KEYS + (2 * a + s) * 2 * KB) for s in range(2)]
            for a in range(PASSES)
        ]
        picked_rows = held([P, S], U8, "picked_rows")

        def gather_words(a, s):
            offsets = picks[:, s * HALF // 16 : (s + 1) * HALF // 16]
            nc.vector.tensor_copy(key_w[a][s][:], tab_w[a][:].bitcast(U32).indirect(offsets))

        def key_scales(a, s):
            return key_s[:, a, s * HALF // 4 : (s + 1) * HALF // 4].bitcast(U8)

        wo_cols = ((0, BANK), (BANK, N))
        wo_raw = [placed([P, PACK, n1 - n0], F32, f"wo_raw{n0}", AT_WO + n0 * 16) for n0, n1 in wo_cols]

        def load_wo(part):
            n0, n1 = wo_cols[part]
            for t in range(PACK):
                load_plane(wo_raw[part], wo[:, n0:n1], t)

        nc.sync.dma_start(picks[:], offs)
        nc.sync.dma_start(tab_rows[0:32, :], tab_scales.bitcast(I32).rearrange("a q w -> q a w"))
        load_words(0)
        nc.sync.dma_start(wg_raw_w[:], wg_words.bitcast(I32).rearrange("a p w -> p a w"))
        for q in range(4):
            nc.sync.dma_start(
                wg_raw_s[32 * q : 32 * q + 4, :, :],
                wg_scales.bitcast(I32)[:, 4 * q : 4 * q + 4, :].rearrange("a r w -> r a w"),
            )
        load_words(1)
        load_wv(0, 0, 2)
        nc.vector.tensor_copy(picked_rows[:], tab_rows[:].bitcast(U8).indirect(picks[:]))
        for q in (0, 2, 1, 3):
            nc.sync.dma_start(key_s[32 * q : 32 * q + 4, :, :], picked_rows[:].bitcast(I32)[8 * q : 8 * q + 8, :])
        load_wv(0, 2, PACK)
        load_wv(1, 0, PACK)
        load_weights(0, 0, HALF)
        nc.sync.dma_start(places[:], offs2)
        for piece in range(1, 4):
            load_weights(*pieces[piece])
        load_wo(0)
        load_weights(2, 0, S)
        load_wo(1)
        load_weights(3, 0, S)
        for t in range(PACK):
            load_plane(base_sb, base, t)

        wg_w = held([P, PASSES, H // 2], I32, "wg_w")
        wg_s = held([P, PASSES, H], U8, "wg_s")
        nc.gpsimd.tensor_copy(
            wg_s[:].rearrange("p a (t u e) -> p a t u e", t=PACK, e=2),
            wg_raw_s[:].bitcast(U8).rearrange("p a (u t e) -> p a t u e", t=PACK, e=2),
        )
        nc.gpsimd.tensor_copy(
            wg_w[:].rearrange("p a (t u) -> p a t u", t=PACK),
            wg_raw_w[:].rearrange("p a (u t) -> p a t u", t=PACK),
        )

        wv_codes = {}

        def round_wv(a, t0, t1, copy):
            rounded = placed([P, t1 - t0, P, PACK], BF16, f"wv_bf{a}_{t0}", AT_ROUNDED + (PACK * a + t0) * KB)
            copy(
                rounded[:].rearrange("p t (u e) j -> p u j t e", e=2),
                wv_raw[a][:].rearrange("p j (u t e) -> p u j t e", t=PACK, e=2)[:, :, :, t0:t1, :],
            )
            return rounded

        def quantize_wv(a, t0, t1, rounded, words):
            scales = held([P, (t1 - t0) * P], U8, f"wv_s{a}_{t0}")
            nc.vector.quantize_mx(
                out=words[:].bitcast(FP8X4), scales=scales[:], in_=rounded[:].rearrange("p t m j -> p (t m j)")
            )
            for t in range(t0, t1):
                cols = slice((t - t0) * P, (t - t0 + 1) * P)
                wv_codes[a, t] = (words[:, cols].bitcast(FP8X4), scales[:, cols])

        def wv_words(a, t0, t1):
            return held([P, (t1 - t0) * P], U32, f"wv_w{a}_{t0}")

        def gate(t, s, at_bank, target):
            acc = bank(at_bank, [P, BANK])
            order = (1, 0)
            for a in order:
                nc.tensor.matmul_mx(
                    out=acc[:],
                    lhsT=wg_w[:, a, t * P // 2 : (t + 1) * P // 2].bitcast(FP4X4),
                    lhsT_scale=wg_s[:, a, t * P : (t + 1) * P],
                    rhs=key_w[a][s][:].bitcast(FP8X4),
                    rhs_scale=key_scales(a, s),
                    start=(a == order[0]),
                    stop=(a == order[-1]),
                )
            nc.scalar.activation(target, acc[:], ACT.Sigmoid)

        def value_pass(acc, t, s, a, start):
            codes, scales = wv_codes[a, t]
            nc.tensor.matmul_mx(
                out=acc[:],
                lhsT=codes,
                lhsT_scale=scales,
                rhs=key_w[a][s][:].bitcast(FP8X4),
                rhs_scale=key_scales(a, s),
                start=start,
                stop=not start,
            )

        def value(t, s, at_bank, target):
            acc = bank(at_bank, [P, BANK])
            value_pass(acc, t, s, 1, True)
            value_pass(acc, t, s, 0, False)
            nc.scalar.copy(target, acc[:])

        def scatter(piece, source):
            t, j0, j1 = pieces[piece]
            nc.vector.tensor_copy(pages[t % 2][:].indirect(places[:, j0 // 16 : j1 // 16]), source)

        gather_words(0, 0)
        gather_words(0, 1)
        gather_words(1, 0)
        gather_words(1, 1)
        rounded = [round_wv(0, t, t + 2, nc.vector.tensor_copy) for t in (0, 2)]
        quantize_wv(0, 0, 2, rounded[0], wv_words(0, 0, 2))
        quantize_wv(0, 2, PACK, rounded[1], wv_words(0, 2, PACK))

        gated = [placed([P, HALF], F32, f"gated{i}", AT_SPARE + i * 2 * KB) for i in range(2)]
        values = [None] + [placed([P, HALF], F32, f"values{i}", AT_VALUES + (i - 1) * 2 * KB) for i in range(1, 4)]
        gate(0, 0, 0, gated[0][:])
        gate(1, 0, 1, gated[1][:])
        early = [bank(3 + t, [P, BANK]) for t in range(2)]
        for t in range(2):
            value_pass(early[t], t, 0, 0, True)
        rounded = [round_wv(1, t, t + 1, nc.vector.tensor_copy) for t in range(2)]
        rounded.append(round_wv(1, 2, PACK, nc.scalar.copy))
        gated.append(placed([P, HALF], F32, "gated2", AT_WV + 14 * KB))
        gated.append(placed([P, HALF], F32, "gated3", AT_SPARE + 4 * KB))
        gated.append(placed([P, S], F32, "gated4", AT_GATED + 2 * KB))
        gated.append(placed([P, S], F32, "gated5", AT_LAST))
        gate(0, 1, 2, gated[2][:])
        for t in range(2):
            quantize_wv(1, t, t + 1, rounded[t], wv_words(1, t, t + 1))
        for t in range(2):
            value_pass(early[t], t, 0, 1, False)
        halves = (slice(0, HALF // 2), slice(HALF // 2, HALF))
        for half in halves:
            nc.vector.tensor_tensor(gated[0][:, half], gated[0][:, half], weights_of(0, 0, HALF)[:, half], MULT)
        first_h = placed([P, HALF], F32, "first_h", AT_GATED)
        for half in halves:
            nc.vector.tensor_tensor(first_h[:, half], early[0][:, half], gated[0][:, half], MULT)
        quantize_wv(1, 2, PACK, rounded[2], placed([P, 2 * P], U32, "wv_late", AT_FIRST_WEIGHTS))
        scatter(0, first_h[:])
        nc.scalar.copy(values[1][:], early[1][:])
        value(0, 1, 0, values[2][:])
        value(1, 1, 1, values[3][:])
        gate(1, 1, 4, gated[3][:])
        for t, gate_banks in ((2, (2, 0)), (3, (1, 3))):
            for s in range(2):
                gate(t, s, gate_banks[s], gated[t + 2][:, s * HALF : (s + 1) * HALF])
        values.extend(placed([P, S], F32, f"values{i}", AT_VALUES + (4 * i - 10) * KB) for i in (4, 5))
        for t, value_banks in ((2, (5, 6)), (3, (7, 2))):
            for s in range(2):
                value(t, s, value_banks[s], values[t + 2][:, s * HALF : (s + 1) * HALF])

        wo_bf = held([P, N, PACK], BF16, "wo_bf")
        for part, (n0, n1) in enumerate(wo_cols):
            nc.scalar.activation(
                wo_bf[:, n0:n1, :].rearrange("p (c i) j -> p c j i", i=4),
                wo_raw[part][:].rearrange("p j (c i) -> p c j i", i=4),
                ACT.Copy,
            )

        def combine(piece):
            t, j0, j1 = pieces[piece]
            weighed = gated[piece]
            if piece == 1:
                weighed = placed([P, HALF], F32, "weighed", AT_FIRST_WEIGHTS + KB)
            nc.gpsimd.tensor_tensor(weighed[:], gated[piece][:], weights_of(t, j0, j1), MULT)
            nc.gpsimd.tensor_tensor(gated[piece][:], weighed[:], values[piece][:], MULT)

        early_factors = [placed([P, PAIRED], F32, f"factors{t}", AT_TAB + t * 8 * KB) for t in range(2)]
        late_factors = placed([P, 2, PAIRED], F32, "late_factors", AT_WV)
        last_factors = held([P, PACK, T2 - PAIRED], F32, "last_factors")

        def factors(t, c0, c1):
            if c0 >= PAIRED:
                return last_factors[:, t, c0 - PAIRED : c1 - PAIRED]
            if t < 2:
                return early_factors[t][:, c0:c1]
            return late_factors[:, t - 2, c0:c1]

        def inverse_root(t, c0, c1, squares):
            nc.scalar.activation(factors(t, c0, c1), squares, ACT.Abs_reciprocal_sqrt, bias=1.0)

        def damp_plane(t):
            squares = placed([P, T2], F32, f"squares{t}", AT_SQUARES)
            nc.scalar.activation(squares[:], pages[t % 2][:], ACT.Square)
            inverse_root(t, 0, PAIRED, squares[:, 0:PAIRED])
            inverse_root(t, PAIRED, T2, squares[:, PAIRED:T2])

        for piece in range(1, len(pieces)):
            combine(piece)
            scatter(piece, gated[piece][:])
            if 2 <= piece < len(pieces) - 1:
                damp_plane(piece - 2)

        pairs = held([P, 2, PAIRED, 2], BF16, "pairs")
        for t in range(2):
            nc.gpsimd.tensor_tensor(pairs[:, 0, :, t], base_sb[:, t, 0:PAIRED], early_factors[t][:], MULT)

        wo_w = placed([P, N], U32, "wo_w", AT_LAST)
        wo_s = held([P, N], U8, "wo_s")
        for n0, n1 in wo_cols:
            nc.vector.quantize_mx(
                out=wo_w[:, n0:n1].bitcast(FP8X4),
                scales=wo_s[:, n0:n1],
                in_=wo_bf[:, n0:n1, :].rearrange("p n j -> p (n j)"),
            )

        steps = [(c, c + STEP // 2) for c in range(0, BANK, STEP // 2)]
        steps.extend((c, c + STEP) for c in range(BANK, T2, STEP))
        z_words = held([P, T2], U32, "z_words")
        z_scales = held([P, T2], U8, "z_scales")

        def z_at(i):
            return AT_FIRST_Z + KB + i * KB if i <= 0 else AT_ROUNDED + steps[i][0] * 8

        def damp_step(i):
            c0, c1 = steps[i]
            at = AT_SQUARES + c0 * 4 if i < AT_ONCE else z_at(i - LAG) + (KB // 2 if i <= LAG else 0)
            squares = placed([P, c1 - c0], F32, f"step_squares{i}", at)
            nc.scalar.activation(squares[:], pages[1][:, c0:c1], ACT.Square)
            inverse_root(PACK - 1, c0, c1, squares[:])

        def form_z(i):
            c0, c1 = steps[i]
            z_bf = placed([P, c1 - c0, PACK], BF16, f"z_bf{i}", z_at(i))
            if c0 >= PAIRED:
                nc.vector.tensor_tensor(
                    z_bf[:].rearrange("p (c i) j -> p c j i", i=2),
                    base_sb[:, :, c0:c1].rearrange("p j (c i) -> p c j i", i=2),
                    last_factors[:, :, c0 - PAIRED : c1 - PAIRED].rearrange("p j (c i) -> p c j i", i=2),
                    MULT,
                )
                return z_bf
            part = slice(c0, c1)
            nc.vector.tensor_tensor(
                pairs[:, 1, part, :].rearrange("p (c i) j -> p c j i", i=4),
                base_sb[:, 2:PACK, c0:c1].rearrange("p j (c i) -> p c j i", i=4),
                late_factors[:, :, part].rearrange("p j (c i) -> p c j i", i=4),
                MULT,
            )
            pair_words = pairs[:].rearrange("p h c j -> p h (c j)").bitcast(I32)
            nc.vector.tensor_copy(
                z_bf[:].bitcast(I32).rearrange("p (c i) h -> p c h i", i=2),
                pair_words[:, :, part].rearrange("p h (c i) -> p c h i", i=2),
            )
            return z_bf

        def quantize_z(i, z_bf):
            c0, c1 = steps[i]
            nc.vector.quantize_mx(
                out=z_words[:, c0:c1].bitcast(FP8X4),
                scales=z_scales[:, c0:c1],
                in_=z_bf[:].rearrange("p c j -> p (c j)"),
            )

        out_rows = out.rearrange("(n p) t -> p n t", p=P)
        starts = [sum(CHUNKS[:c]) for c in range(len(CHUNKS))]
        filled = []

        def project(c):
            width = CHUNKS[c]
            cols = slice(starts[c], starts[c] + width)
            per_bank = 2 if width < BANK else 1
            for i in range(N // P // per_bank):
                n0 = i * per_bank
                joined = 2 if per_bank == 1 and (c, i) < (len(CHUNKS) - 1, 4) else 1
                if i % joined == 0:
                    at = AT_WEIGHTS + sum(filled)
                    staged = placed([P, joined * per_bank, width], F32, f"result{len(filled)}", at)
                result = staged[:, (i % joined) * per_bank : (i % joined + 1) * per_bank, :]
                acc = bank(len(filled) % BANKS, [P, per_bank, width])
                filled.append(per_bank * width * 4)
                for n in range(per_bank):
                    rows = slice((n0 + n) * P, (n0 + n + 1) * P)
                    nc.tensor.matmul_mx(
                        out=acc[:, n, :],
                        lhsT=wo_w[:, rows].bitcast(FP8X4),
                        lhsT_scale=wo_s[:, rows],
                        rhs=z_words[:, cols].bitcast(FP8X4),
                        rhs_scale=z_scales[:, cols],
                        start=True,
                        stop=True,
                    )
                if i in VECTOR_BANKS[c]:
                    nc.vector.tensor_copy(result, acc[:])
                else:
                    nc.scalar.copy(result, acc[:])
                if i % joined == joined - 1:
                    first = n0 - (joined - 1) * per_bank
                    nc.sync.dma_start(out_rows[:, first : n0 + per_bank, cols], staged[:])

        for i in range(4):
            damp_step(i)
        quantize_z(0, form_z(0))
        done = 1
        damped = 4
        for c in range(len(CHUNKS)):
            ahead = starts[c + 1] + CHUNKS[c + 1] if c + 1 < len(CHUNKS) else T2
            while done < len(steps) and steps[done][1] <= ahead:
                while damped <= done:
                    damp_step(damped)
                    damped = damped + 1
                quantize_z(done, form_z(done))
                done = done + 1
            project(c)
